import numpy as np
import ml_dtypes


def mxq(x, axis, fmt="e4m3"):
    dtype, down = {"e4m3": (ml_dtypes.float8_e4m3fn, 7), "e5m2": (ml_dtypes.float8_e5m2, 14)}[fmt]
    v = np.moveaxis(np.asarray(x, np.float32).astype(ml_dtypes.bfloat16).astype(np.float64), axis, -1)
    blocks = v.reshape(v.shape[:-1] + (-1, 32))
    amax = np.abs(blocks).max(-1, keepdims=True)
    byte = np.maximum(np.where(amax > 0, np.frexp(amax)[1] - 1 + 127, 0) - down, 1)
    scale = np.exp2(byte - 127.0)
    codes = (blocks / scale).astype(np.float32).astype(dtype).astype(np.float64)
    return np.moveaxis((codes * scale).reshape(v.shape), -1, axis)


WIDE = False


def mx_kscale(k):
    if not WIDE:
        return np.ones(k)
    levels = np.array([10, -10, 5, -5, 0])
    if k % 512:
        return np.exp2(np.random.permutation(np.resize(levels, k // 32))).repeat(32)
    a = np.empty((k // 512, 16))
    for p in range(k // 512):
        a[p, :8] = np.random.permutation(np.resize(levels, 8))
        for g in range(8):
            far = levels[np.abs(levels - a[p, g]) >= 10]
            a[p, g + 8] = far[np.random.randint(len(far))]
    return np.exp2(a.ravel()).repeat(32)


def f64(x):
    return np.asarray(x).astype(np.float64)


def striped(idx):
    return np.tile(idx.reshape(-1, 16).T, (8, 1)).astype(np.uint16)


def unstriped(offs):
    return offs[:16].T.reshape(-1).astype(np.int64)


def pack_weight(w):
    k, n = w.shape
    w = f64(np.asarray(w, np.float32).astype(ml_dtypes.bfloat16)).reshape(k // 32, 32, n)
    amax = np.abs(w).max(1)
    byte = np.clip(np.where(amax > 0, np.frexp(amax)[1] - 1 + 127 - 7, 1), 1, 254)
    scaled = (w * np.exp2(127.0 - byte)[:, None, :]).reshape(k, n).astype(np.float32)
    words = np.ascontiguousarray(scaled.reshape(k // 512, 128, 4, n).transpose(0, 1, 3, 2)).astype(ml_dtypes.float8_e4m3fn).view(np.uint8)
    return words, np.ascontiguousarray(byte.astype(np.uint8).reshape(k // 512, 16, n))


def unpack_weight(words, scales):
    g, p, n, _ = words.shape
    vals = np.ascontiguousarray(words).view(ml_dtypes.float8_e4m3fn).astype(np.float64) * np.repeat(np.exp2(scales.astype(np.float64) - 127.0), 8, axis=1)[..., None]
    return vals.transpose(0, 1, 3, 2).reshape(g * 512, n)


def gelu(v):
    return 0.5 * v * (1.0 + np.tanh(np.sqrt(2.0 / np.pi) * (v + 0.044715 * v**3)))


K, T, E, C, N = 1024, 640, 4, 128, 128


def by_expert(wq, xq):
    return np.concatenate([wq[e].T @ xq[:, e * C:(e + 1) * C] for e in range(E)], axis=1)


def setup_inputs():
    n = np.random.standard_normal
    s = mx_kscale(K)[:, None]
    packed = [pack_weight(m) for m in n((E, K, N)) / np.sqrt(K) / s[None]]
    return {
        "xT": (n((K, T)) * s).astype(np.float32),
        "w_words": np.stack([m[0] for m in packed]),
        "w_scales": np.stack([m[1] for m in packed]),
        "b": (0.3 * n((N, E))).astype(np.float32),
        "gate": np.tile(np.random.uniform(0.2, 1.0, E * C), (N, 1)).astype(np.float32),
        "offs": striped(np.random.permutation(T)[:E * C]),
        "dst": striped(np.random.permutation(T)[:E * C]),
    }


def reference(xT, w_words, w_scales, b, gate, offs, dst):
    idx = unstriped(offs)
    w = np.stack([unpack_weight(w_words[e], w_scales[e]) for e in range(E)])
    xq = mxq(f64(xT)[:, idx], 0, "e4m3")
    y = by_expert(w, xq)
    y = gelu(y + np.repeat(f64(b), C, axis=1))
    out = np.zeros((N, T))
    out[:, unstriped(dst)] = f64(gate) * y
    return out

@@ -1,0 +1,162 @@
+from contextlib import ExitStack
+
+import concourse.mybir as mybir
+
+K, T, E, C, N = 1024, 640, 4, 128, 128
+P = 128
+S = E * C
+FLOPS = 2 * S * K * N
+
+F32 = mybir.dt.float32
+BF16 = mybir.dt.bfloat16
+U32 = mybir.dt.uint32
+I32 = mybir.dt.int32
+U16 = mybir.dt.uint16
+U8 = mybir.dt.uint8
+FP8X4 = mybir.dt.float8_e4m3fn_x4
+GELU = mybir.ActivationFunctionType.Gelu_apprx_tanh
+COPY = mybir.ActivationFunctionType.Copy
+MULT = mybir.AluOpType.mult
+
+CHUNKS = (
+    (0, 0, 640, 0, (512, 128)),
+    (1, 0, 256, 0, (256,)),
+    (1, 256, 256, 96, (256,)),
+    (1, 512, 128, 80, (128,)),
+)
+
+
+def tile_moe_two_lin_gelu_kernel(tc, xT, w_words, w_scales, b, gate, offs, dst, out):
+    nc = tc.nc
+    with ExitStack() as ctx:
+        keep = ctx.enter_context(tc.tile_pool(name="keep", bufs=1))
+        psum = ctx.enter_context(tc.psum_pool(name="psum", bufs=1))
+
+        offs_t = keep.tile([P, S // 16], U16, name="offs_t")
+        dst_t = keep.tile([P, S // 16], U16, name="dst_t")
+        b_t = keep.tile([P, E], F32, name="b_t")
+
+        raws = []
+        for i, (a, t0, n, nv, qs) in enumerate(CHUNKS):
+            raw = keep.tile([P, 4, n], F32, name=f"raw{i}")
+            nc.sync.dma_start(
+                raw[:],
+                xT[512 * a : 512 * (a + 1), t0 : t0 + n].rearrange("(p j) t -> p j t", j=4),
+            )
+            raws.append(raw)
+            if i == 0:
+                nc.sync.dma_start(offs_t[:], offs)
+
+        ws = keep.tile([P, 2 * E, N], U8, name="ws", align_bytes=64)
+        nc.vector.memset(ws[:].rearrange("p g n -> p (g n)").bitcast(I32), 0)
+        for q in range(4):
+            nc.scalar.dma_start(
+                ws[32 * q : 32 * q + 4, :, :].bitcast(I32),
+                w_scales[:, :, 4 * q : 4 * q + 4, :].rearrange("e a q n -> q (e a) n").bitcast(I32),
+            )
+        xs = keep.tile([P, T], U8, name="xs", align_bytes=64)
+        nc.gpsimd.memset(xs[:], 0)
+        o_t = keep.tile([P, T], F32, name="o_t")
+        nc.vector.memset(o_t[:], 0.0)
+        warm = keep.tile([P, 1], F32, name="warm")
+        nc.vector.memset(warm[:], 0.0)
+        nc.scalar.activation(warm[:], warm[:], GELU)
+
+        ww = []
+        for h in range(2):
+            w_t = keep.tile([P, 4, N], I32, name=f"w{h}", align_bytes=64)
+            nc.sync.dma_start(
+                w_t[:],
+                w_words[2 * h : 2 * h + 2].rearrange("e a p n r -> p (e a) (n r)").bitcast(I32),
+            )
+            ww.append(w_t)
+        nc.sync.dma_start(b_t[:], b)
+        gate_t = keep.tile([P, S], F32, name="gate_t")
+        nc.sync.dma_start(gate_t[:], gate)
+        nc.sync.dma_start(dst_t[:], dst)
+
+        xw = [keep.tile([P, T], U32, name=f"xw{a}", align_bytes=64) for a in range(2)]
+        gw = [[keep.tile([P, 2 * C], U32, name=f"gw{a}{h}", align_bytes=64) for h in range(2)] for a in range(2)]
+        gb = [keep.tile([P, 2 * C], U8, name=f"gb{h}", align_bytes=64) for h in range(2)]
+
+        def cast(i):
+            a, t0, n, nv, qs = CHUNKS[i]
+            g = keep.tile([P, n, 4], BF16, name=f"g{i}", align_bytes=64)
+            src = raws[i][:].rearrange("p j t -> p t j")
+            if nv > 0:
+                nc.vector.tensor_copy(g[:, 0:nv, :], src[:, 0:nv, :])
+            nc.scalar.activation(g[:, nv:n, :], src[:, nv:n, :], COPY)
+            return g
+
+        def quantize(i, g):
+            a, t0, n, nv, qs = CHUNKS[i]
+            s = 0
+            for w in qs:
+                cols = slice(t0 + s, t0 + s + w)
+                nc.vector.quantize_mx(
+                    out=xw[a][:, cols].bitcast(FP8X4),
+                    scales=xs[4 * a : P, cols],
+                    in_=g[:, s : s + w, :].rearrange("p t j -> p (t j)"),
+                )
+                s += w
+
+        def list_of(tile, h):
+            return tile[:, 16 * h : 16 * h + 16]
+
+        def gather_words(a, h):
+            nc.vector.tensor_copy(gw[a][h][:], xw[a][:].indirect(list_of(offs_t, h)))
+
+        def gather_bytes(h):
+            nc.vector.tensor_copy(gb[h][:], xs[:].indirect(list_of(offs_t, h)))
+
+        g0 = []
+        for t0, n, nv in ((0, 512, 336), (512, 128, 80)):
+            g = keep.tile([P, n, 4], BF16, name=f"g0{t0}", align_bytes=64)
+            src = raws[0][:].rearrange("p j t -> p t j")
+            nc.vector.tensor_copy(g[:, 0:nv, :], src[:, t0 : t0 + nv, :])
+            nc.scalar.activation(g[:, nv:n, :], src[:, t0 + nv : t0 + n, :], COPY)
+            g0.append((t0, n, g))
+        for t0, n, g in g0:
+            nc.vector.quantize_mx(
+                out=xw[0][:, t0 : t0 + n].bitcast(FP8X4),
+                scales=xs[:, t0 : t0 + n],
+                in_=g[:].rearrange("p t j -> p (t j)"),
+            )
+        g1 = cast(1)
+        gather_words(0, 0)
+        gather_words(0, 1)
+        quantize(1, g1)
+        g2 = cast(2)
+        g3 = cast(3)
+        quantize(2, g2)
+        quantize(3, g3)
+
+        ys = []
+        for h in range(2):
+            y = keep.tile([P, 2 * C], F32, name=f"y{h}")
+            ys.append(y)
+            gather_bytes(h)
+            gather_words(1, h)
+            for e in (2 * h, 2 * h + 1):
+                c = slice((e - 2 * h) * C, (e - 2 * h + 1) * C)
+                ps = psum.tile([P, C], F32, name=f"ps{e}")
+                for a in range(2):
+                    nc.tensor.matmul_mx(
+                        out=ps[:],
+                        lhsT=ww[h][:, 2 * (e - 2 * h) + a, :].bitcast(FP8X4),
+                        lhsT_scale=ws[:, 2 * e + a, :],
+                        rhs=gw[a][h][:, c].bitcast(FP8X4),
+                        rhs_scale=gb[h][4 * a : P, c],
+                        start=(a == 0),
+                        stop=(a == 1),
+                    )
+                nc.scalar.activation(y[:, c], ps[:], GELU, bias=b_t[:, e : e + 1])
+
+        for h in range(2):
+            nc.vector.tensor_tensor(
+                o_t[:].indirect(list_of(dst_t, h)),
+                ys[h][:],
+                gate_t[:, 2 * h * C : 2 * (h + 1) * C],
+                MULT,
+            )
+        nc.sync.dma_start(out, o_t[:])

@@ -79,13 +79,20 @@ def tile_moe_two_lin_gelu_kernel(tc, xT, w_words, w_scales, b, gate, offs, dst, 
         gw = [[keep.tile([P, 2 * C], U32, name=f"gw{a}{h}", align_bytes=64) for h in range(2)] for a in range(2)]
         gb = [keep.tile([P, 2 * C], U8, name=f"gb{h}", align_bytes=64) for h in range(2)]
 
+        def weave(on_vector, to, rows):
+            to = to.rearrange("p (c i) j -> p c j i", i=4)
+            rows = rows.rearrange("p j (c i) -> p c j i", i=4)
+            if on_vector:
+                nc.vector.tensor_copy(to, rows)
+            else:
+                nc.scalar.activation(to, rows, COPY)
+
         def cast(i):
             a, t0, n, nv, qs = CHUNKS[i]
             g = keep.tile([P, n, 4], BF16, name=f"g{i}", align_bytes=64)
-            src = raws[i][:].rearrange("p j t -> p t j")
             if nv > 0:
-                nc.vector.tensor_copy(g[:, 0:nv, :], src[:, 0:nv, :])
-            nc.scalar.activation(g[:, nv:n, :], src[:, nv:n, :], COPY)
+                weave(True, g[:, 0:nv, :], raws[i][:, :, 0:nv])
+            weave(False, g[:, nv:n, :], raws[i][:, :, nv:n])
             return g
 
         def quantize(i, g):
@@ -112,9 +119,8 @@ def tile_moe_two_lin_gelu_kernel(tc, xT, w_words, w_scales, b, gate, offs, dst, 
         g0 = []
         for t0, n, nv in ((0, 512, 336), (512, 128, 80)):
             g = keep.tile([P, n, 4], BF16, name=f"g0{t0}", align_bytes=64)
-            src = raws[0][:].rearrange("p j t -> p t j")
-            nc.vector.tensor_copy(g[:, 0:nv, :], src[:, t0 : t0 + nv, :])
-            nc.scalar.activation(g[:, nv:n, :], src[:, t0 + nv : t0 + n, :], COPY)
+            weave(True, g[:, 0:nv, :], raws[0][:, :, t0 : t0 + nv])
+            weave(False, g[:, nv:n, :], raws[0][:, :, t0 + nv : t0 + n])
             g0.append((t0, n, g))
         for t0, n, g in g0:
             nc.vector.quantize_mx(

@@ -19,11 +19,13 @@ COPY = mybir.ActivationFunctionType.Copy
 MULT = mybir.AluOpType.mult
 
 CHUNKS = (
-    (0, 0, 640, 0, (512, 128)),
-    (1, 0, 256, 0, (256,)),
-    (1, 256, 256, 96, (256,)),
-    (1, 512, 128, 80, (128,)),
+    (0, 0, 384, 192, (256, 128)),
+    (0, 384, 256, 160, (256,)),
+    (1, 0, 256, 96, (256,)),
+    (1, 256, 256, 128, (256,)),
+    (1, 512, 128, 64, (128,)),
 )
+WINDOW = 704
 
 
 def tile_moe_two_lin_gelu_kernel(tc, xT, w_words, w_scales, b, gate, offs, dst, out):
@@ -44,18 +46,13 @@ def tile_moe_two_lin_gelu_kernel(tc, xT, w_words, w_scales, b, gate, offs, dst, 
                 xT[512 * a : 512 * (a + 1), t0 : t0 + n].rearrange("(p j) t -> p j t", j=4),
             )
             raws.append(raw)
-            if i == 0:
+            if i == 1:
                 nc.sync.dma_start(offs_t[:], offs)
 
         ws = keep.tile([P, 2 * E, N], U8, name="ws", align_bytes=64)
-        nc.vector.memset(ws[:].rearrange("p g n -> p (g n)").bitcast(I32), 0)
-        for q in range(4):
-            nc.scalar.dma_start(
-                ws[32 * q : 32 * q + 4, :, :].bitcast(I32),
-                w_scales[:, :, 4 * q : 4 * q + 4, :].rearrange("e a q n -> q (e a) n").bitcast(I32),
-            )
+        nc.gpsimd.memset(ws[:].rearrange("p g n -> p (g n)").bitcast(I32), 0)
         xs = keep.tile([P, T], U8, name="xs", align_bytes=64)
-        nc.gpsimd.memset(xs[:], 0)
+        nc.vector.memset(xs[:].bitcast(I32), 0)
         o_t = keep.tile([P, T], F32, name="o_t")
         nc.vector.memset(o_t[:], 0.0)
         warm = keep.tile([P, 1], F32, name="warm")
@@ -70,13 +67,22 @@ def tile_moe_two_lin_gelu_kernel(tc, xT, w_words, w_scales, b, gate, offs, dst, 
                 w_words[2 * h : 2 * h + 2].rearrange("e a p n r -> p (e a) (n r)").bitcast(I32),
             )
             ww.append(w_t)
-        nc.sync.dma_start(b_t[:], b)
+            if h == 0:
+                for q in range(4):
+                    nc.sync.dma_start(
+                        ws[32 * q : 32 * q + 4, :, :].bitcast(I32),
+                        w_scales[:, :, 4 * q : 4 * q + 4, :].rearrange("e a q n -> q (e a) n").bitcast(I32),
+                    )
+                nc.sync.dma_start(b_t[:], b)
         gate_t = keep.tile([P, S], F32, name="gate_t")
         nc.sync.dma_start(gate_t[:], gate)
         nc.sync.dma_start(dst_t[:], dst)
 
-        xw = [keep.tile([P, T], U32, name=f"xw{a}", align_bytes=64) for a in range(2)]
-        gw = [[keep.tile([P, 2 * C], U32, name=f"gw{a}{h}", align_bytes=64) for h in range(2)] for a in range(2)]
+        xw = [keep.tile([P, n], U32, name=f"xw{a}", align_bytes=64) for a, n in enumerate((WINDOW, T))]
+        nc.vector.memset(xw[0][:, T:WINDOW].bitcast(I32), 0)
+        gw0 = keep.tile([P, S], U32, name="gw0", align_bytes=64)
+        gw1 = [keep.tile([P, 2 * C], U32, name=f"gw1{h}", align_bytes=64) for h in range(2)]
+        gw = [[gw0[:, 0 : 2 * C], gw0[:, 2 * C : S]], [gw1[0][:], gw1[1][:]]]
         gb = [keep.tile([P, 2 * C], U8, name=f"gb{h}", align_bytes=64) for h in range(2)]
 
         def weave(on_vector, to, rows):
@@ -111,31 +117,20 @@ def tile_moe_two_lin_gelu_kernel(tc, xT, w_words, w_scales, b, gate, offs, dst, 
             return tile[:, 16 * h : 16 * h + 16]
 
         def gather_words(a, h):
-            nc.vector.tensor_copy(gw[a][h][:], xw[a][:].indirect(list_of(offs_t, h)))
+            nc.vector.tensor_copy(gw[a][h], xw[a][:].indirect(list_of(offs_t, h)))
 
         def gather_bytes(h):
             nc.vector.tensor_copy(gb[h][:], xs[:].indirect(list_of(offs_t, h)))
 
-        g0 = []
-        for t0, n, nv in ((0, 512, 336), (512, 128, 80)):
-            g = keep.tile([P, n, 4], BF16, name=f"g0{t0}", align_bytes=64)
-            weave(True, g[:, 0:nv, :], raws[0][:, :, t0 : t0 + nv])
-            weave(False, g[:, nv:n, :], raws[0][:, :, t0 + nv : t0 + n])
-            g0.append((t0, n, g))
-        for t0, n, g in g0:
-            nc.vector.quantize_mx(
-                out=xw[0][:, t0 : t0 + n].bitcast(FP8X4),
-                scales=xs[:, t0 : t0 + n],
-                in_=g[:].rearrange("p t j -> p (t j)"),
-            )
-        g1 = cast(1)
-        gather_words(0, 0)
-        gather_words(0, 1)
-        quantize(1, g1)
+        quantize(0, cast(0))
+        quantize(1, cast(1))
         g2 = cast(2)
-        g3 = cast(3)
+        nc.vector.tensor_copy(gw0[:], xw[0][:].indirect(offs_t[:]))
         quantize(2, g2)
+        g3 = cast(3)
+        g4 = cast(4)
         quantize(3, g3)
+        quantize(4, g4)
 
         ys = []
         for h in range(2):
@@ -143,20 +138,22 @@ def tile_moe_two_lin_gelu_kernel(tc, xT, w_words, w_scales, b, gate, offs, dst, 
             ys.append(y)
             gather_bytes(h)
             gather_words(1, h)
-            for e in (2 * h, 2 * h + 1):
-                c = slice((e - 2 * h) * C, (e - 2 * h + 1) * C)
-                ps = psum.tile([P, C], F32, name=f"ps{e}")
-                for a in range(2):
+            ps = [psum.tile([P, C], F32, name=f"ps{2 * h + i}") for i in range(2)]
+            for a in range(2):
+                for i in range(2):
+                    c = slice(i * C, (i + 1) * C)
                     nc.tensor.matmul_mx(
-                        out=ps[:],
-                        lhsT=ww[h][:, 2 * (e - 2 * h) + a, :].bitcast(FP8X4),
-                        lhsT_scale=ws[:, 2 * e + a, :],
+                        out=ps[i][:],
+                        lhsT=ww[h][:, 2 * i + a, :].bitcast(FP8X4),
+                        lhsT_scale=ws[:, 2 * (2 * h + i) + a, :],
                         rhs=gw[a][h][:, c].bitcast(FP8X4),
                         rhs_scale=gb[h][4 * a : P, c],
                         start=(a == 0),
                         stop=(a == 1),
                     )
-                nc.scalar.activation(y[:, c], ps[:], GELU, bias=b_t[:, e : e + 1])
+            for i in range(2):
+                e = 2 * h + i
+                nc.scalar.activation(y[:, i * C : (i + 1) * C], ps[i][:], GELU, bias=b_t[:, e : e + 1])
 
         for h in range(2):
             nc.vector.tensor_tensor(

@@ -18,13 +18,8 @@ GELU = mybir.ActivationFunctionType.Gelu_apprx_tanh
 COPY = mybir.ActivationFunctionType.Copy
 MULT = mybir.AluOpType.mult
 
-CHUNKS = (
-    (0, 0, 384, 192, (256, 128)),
-    (0, 384, 256, 160, (256,)),
-    (1, 0, 256, 96, (256,)),
-    (1, 256, 256, 128, (256,)),
-    (1, 512, 128, 64, (128,)),
-)
+CHUNKS = ((0, 0, 384), (0, 384, 256), (1, 0, 256), (1, 256, 192), (1, 448, 192))
+PIECES = (((0, 256), (256, 128), (384, 256)), ((0, 256), (256, 256), (512, 128)))
 WINDOW = 704
 
 
@@ -39,8 +34,8 @@ def tile_moe_two_lin_gelu_kernel(tc, xT, w_words, w_scales, b, gate, offs, dst, 
         b_t = keep.tile([P, E], F32, name="b_t")
 
         raws = []
-        for i, (a, t0, n, nv, qs) in enumerate(CHUNKS):
-            raw = keep.tile([P, 4, n], F32, name=f"raw{i}")
+        for i, (a, t0, n) in enumerate(CHUNKS):
+            raw = keep.tile([P, 4, n], F32, name=f"raw{i}", tag=f"raw{i}")
             nc.sync.dma_start(
                 raw[:],
                 xT[512 * a : 512 * (a + 1), t0 : t0 + n].rearrange("(p j) t -> p j t", j=4),
@@ -50,32 +45,23 @@ def tile_moe_two_lin_gelu_kernel(tc, xT, w_words, w_scales, b, gate, offs, dst, 
                 nc.sync.dma_start(offs_t[:], offs)
 
         ws = keep.tile([P, 2 * E, N], U8, name="ws", align_bytes=64)
-        nc.gpsimd.memset(ws[:].rearrange("p g n -> p (g n)").bitcast(I32), 0)
+        nc.vector.memset(ws[:].rearrange("p g n -> p (g n)").bitcast(I32), 0)
         xs = keep.tile([P, T], U8, name="xs", align_bytes=64)
-        nc.vector.memset(xs[:].bitcast(I32), 0)
+        nc.gpsimd.memset(xs[:].bitcast(I32), 0)
         o_t = keep.tile([P, T], F32, name="o_t")
         nc.vector.memset(o_t[:], 0.0)
         warm = keep.tile([P, 1], F32, name="warm")
         nc.vector.memset(warm[:], 0.0)
         nc.scalar.activation(warm[:], warm[:], GELU)
 
-        ww = []
-        for h in range(2):
-            w_t = keep.tile([P, 4, N], I32, name=f"w{h}", align_bytes=64)
+        ww = keep.tile([P, 2 * E, N], I32, name="ww", align_bytes=64)
+        nc.sync.dma_start(ww[:], w_words.rearrange("e a p n r -> p (e a) (n r)").bitcast(I32))
+        for q in range(4):
             nc.sync.dma_start(
-                w_t[:],
-                w_words[2 * h : 2 * h + 2].rearrange("e a p n r -> p (e a) (n r)").bitcast(I32),
+                ws[32 * q : 32 * q + 4, :, :].bitcast(I32),
+                w_scales[:, :, 4 * q : 4 * q + 4, :].rearrange("e a q n -> q (e a) n").bitcast(I32),
             )
-            ww.append(w_t)
-            if h == 0:
-                for q in range(4):
-                    nc.sync.dma_start(
-                        ws[32 * q : 32 * q + 4, :, :].bitcast(I32),
-                        w_scales[:, :, 4 * q : 4 * q + 4, :].rearrange("e a q n -> q (e a) n").bitcast(I32),
-                    )
-                nc.sync.dma_start(b_t[:], b)
-        gate_t = keep.tile([P, S], F32, name="gate_t")
-        nc.sync.dma_start(gate_t[:], gate)
+        nc.sync.dma_start(b_t[:], b)
         nc.sync.dma_start(dst_t[:], dst)
 
         xw = [keep.tile([P, n], U32, name=f"xw{a}", align_bytes=64) for a, n in enumerate((WINDOW, T))]
@@ -93,25 +79,23 @@ def tile_moe_two_lin_gelu_kernel(tc, xT, w_words, w_scales, b, gate, offs, dst, 
             else:
                 nc.scalar.activation(to, rows, COPY)
 
-        def cast(i):
-            a, t0, n, nv, qs = CHUNKS[i]
-            g = keep.tile([P, n, 4], BF16, name=f"g{i}", align_bytes=64)
-            if nv > 0:
-                weave(True, g[:, 0:nv, :], raws[i][:, :, 0:nv])
-            weave(False, g[:, nv:n, :], raws[i][:, :, nv:n])
-            return g
+        g = [
+            [keep.tile([P, n, 4], BF16, name=f"g{a}{i}", align_bytes=64) for i, (t0, n) in enumerate(PIECES[a])]
+            for a in range(2)
+        ]
 
-        def quantize(i, g):
-            a, t0, n, nv, qs = CHUNKS[i]
-            s = 0
-            for w in qs:
-                cols = slice(t0 + s, t0 + s + w)
-                nc.vector.quantize_mx(
-                    out=xw[a][:, cols].bitcast(FP8X4),
-                    scales=xs[4 * a : P, cols],
-                    in_=g[:, s : s + w, :].rearrange("p t j -> p (t j)"),
-                )
-                s += w
+        def cast(on_vector, a, lo, hi):
+            (r0, raw), = [(t0, raws[i]) for i, (b0, t0, n) in enumerate(CHUNKS) if b0 == a and t0 <= lo < t0 + n]
+            (p0, piece), = [(t0, g[a][i]) for i, (t0, n) in enumerate(PIECES[a]) if t0 <= lo < t0 + n]
+            weave(on_vector, piece[:, lo - p0 : hi - p0, :], raw[:, :, lo - r0 : hi - r0])
+
+        def quantize(a, i):
+            t0, n = PIECES[a][i]
+            nc.vector.quantize_mx(
+                out=xw[a][:, t0 : t0 + n].bitcast(FP8X4),
+                scales=xs[4 * a : P, t0 : t0 + n],
+                in_=g[a][i][:].rearrange("p t j -> p (t j)"),
+            )
 
         def list_of(tile, h):
             return tile[:, 16 * h : 16 * h + 16]
@@ -122,15 +106,25 @@ def tile_moe_two_lin_gelu_kernel(tc, xT, w_words, w_scales, b, gate, offs, dst, 
         def gather_bytes(h):
             nc.vector.tensor_copy(gb[h][:], xs[:].indirect(list_of(offs_t, h)))
 
-        quantize(0, cast(0))
-        quantize(1, cast(1))
-        g2 = cast(2)
+        cast(True, 0, 0, 256)
+        cast(False, 0, 256, 384)
+        gate_t = keep.tile([P, S], F32, name="gate_t", tag="raw0")
+        nc.sync.dma_start(gate_t[:], gate)
+        quantize(0, 0)
+        quantize(0, 1)
+        cast(True, 0, 384, 544)
+        cast(False, 0, 544, 640)
+        quantize(0, 2)
+        cast(False, 1, 0, 256)
         nc.vector.tensor_copy(gw0[:], xw[0][:].indirect(offs_t[:]))
-        quantize(2, g2)
-        g3 = cast(3)
-        g4 = cast(4)
-        quantize(3, g3)
-        quantize(4, g4)
+        quantize(1, 0)
+        cast(True, 1, 256, 320)
+        cast(False, 1, 320, 448)
+        cast(True, 1, 448, 512)
+        cast(True, 1, 512, 576)
+        cast(False, 1, 576, 640)
+        quantize(1, 1)
+        quantize(1, 2)
 
         ys = []
         for h in range(2):
@@ -144,7 +138,7 @@ def tile_moe_two_lin_gelu_kernel(tc, xT, w_words, w_scales, b, gate, offs, dst, 
                     c = slice(i * C, (i + 1) * C)
                     nc.tensor.matmul_mx(
                         out=ps[i][:],
-                        lhsT=ww[h][:, 2 * i + a, :].bitcast(FP8X4),
+                        lhsT=ww[:, 2 * (2 * h + i) + a, :].bitcast(FP8X4),
                         lhsT_scale=ws[:, 2 * (2 * h + i) + a, :],
                         rhs=gw[a][h][:, c].bitcast(FP8X4),
                         rhs_scale=gb[h][4 * a : P, c],

@@ -54,14 +54,22 @@ def tile_moe_two_lin_gelu_kernel(tc, xT, w_words, w_scales, b, gate, offs, dst, 
         nc.vector.memset(warm[:], 0.0)
         nc.scalar.activation(warm[:], warm[:], GELU)
 
-        ww = keep.tile([P, 2 * E, N], I32, name="ww", align_bytes=64)
-        nc.sync.dma_start(ww[:], w_words.rearrange("e a p n r -> p (e a) (n r)").bitcast(I32))
+        def load_words(h):
+            w_t = keep.tile([P, 4, N], I32, name=f"w{h}", align_bytes=64)
+            nc.sync.dma_start(
+                w_t[:],
+                w_words[2 * h : 2 * h + 2].rearrange("e a p n r -> p (e a) (n r)").bitcast(I32),
+            )
+            return w_t
+
+        ww = [load_words(0)]
         for q in range(4):
             nc.sync.dma_start(
                 ws[32 * q : 32 * q + 4, :, :].bitcast(I32),
                 w_scales[:, :, 4 * q : 4 * q + 4, :].rearrange("e a q n -> q (e a) n").bitcast(I32),
             )
         nc.sync.dma_start(b_t[:], b)
+        ww.append(load_words(1))
         nc.sync.dma_start(dst_t[:], dst)
 
         xw = [keep.tile([P, n], U32, name=f"xw{a}", align_bytes=64) for a, n in enumerate((WINDOW, T))]
@@ -138,7 +146,7 @@ def tile_moe_two_lin_gelu_kernel(tc, xT, w_words, w_scales, b, gate, offs, dst, 
                     c = slice(i * C, (i + 1) * C)
                     nc.tensor.matmul_mx(
                         out=ps[i][:],
-                        lhsT=ww[:, 2 * (2 * h + i) + a, :].bitcast(FP8X4),
+                        lhsT=ww[h][:, 2 * i + a, :].bitcast(FP8X4),
                         lhsT_scale=ws[:, 2 * (2 * h + i) + a, :],
                         rhs=gw[a][h][:, c].bitcast(FP8X4),
                         rhs_scale=gb[h][4 * a : P, c],

@@ -18,8 +18,8 @@ GELU = mybir.ActivationFunctionType.Gelu_apprx_tanh
 COPY = mybir.ActivationFunctionType.Copy
 MULT = mybir.AluOpType.mult
 
-CHUNKS = ((0, 0, 384), (0, 384, 256), (1, 0, 256), (1, 256, 192), (1, 448, 192))
-PIECES = (((0, 256), (256, 128), (384, 256)), ((0, 256), (256, 256), (512, 128)))
+CHUNKS = ((0, 0, 2, 0, 640), (0, 2, 2, 0, 640), (1, 0, 4, 0, 256), (1, 0, 4, 256, 192), (1, 0, 4, 448, 192))
+PIECES = (((0, 256), (256, 256), (512, 128)), ((0, 256), (256, 256), (512, 128)))
 WINDOW = 704
 
 
@@ -34,12 +34,10 @@ def tile_moe_two_lin_gelu_kernel(tc, xT, w_words, w_scales, b, gate, offs, dst, 
         b_t = keep.tile([P, E], F32, name="b_t")
 
         raws = []
-        for i, (a, t0, n) in enumerate(CHUNKS):
-            raw = keep.tile([P, 4, n], F32, name=f"raw{i}", tag=f"raw{i}")
-            nc.sync.dma_start(
-                raw[:],
-                xT[512 * a : 512 * (a + 1), t0 : t0 + n].rearrange("(p j) t -> p j t", j=4),
-            )
+        for i, (a, j0, nj, t0, n) in enumerate(CHUNKS):
+            raw = keep.tile([P, nj, n], F32, name=f"raw{i}", tag=f"raw{i}")
+            rows = xT[512 * a : 512 * (a + 1), t0 : t0 + n].rearrange("(p j) t -> p j t", j=4)
+            nc.sync.dma_start(raw[:], rows[:, j0 : j0 + nj, :])
             raws.append(raw)
             if i == 1:
                 nc.sync.dma_start(offs_t[:], offs)
@@ -79,23 +77,25 @@ def tile_moe_two_lin_gelu_kernel(tc, xT, w_words, w_scales, b, gate, offs, dst, 
         gw = [[gw0[:, 0 : 2 * C], gw0[:, 2 * C : S]], [gw1[0][:], gw1[1][:]]]
         gb = [keep.tile([P, 2 * C], U8, name=f"gb{h}", align_bytes=64) for h in range(2)]
 
-        def weave(on_vector, to, rows):
-            to = to.rearrange("p (c i) j -> p c j i", i=4)
-            rows = rows.rearrange("p j (c i) -> p c j i", i=4)
-            if on_vector:
-                nc.vector.tensor_copy(to, rows)
-            else:
-                nc.scalar.activation(to, rows, COPY)
-
         g = [
             [keep.tile([P, n, 4], BF16, name=f"g{a}{i}", align_bytes=64) for i, (t0, n) in enumerate(PIECES[a])]
             for a in range(2)
         ]
 
-        def cast(on_vector, a, lo, hi):
-            (r0, raw), = [(t0, raws[i]) for i, (b0, t0, n) in enumerate(CHUNKS) if b0 == a and t0 <= lo < t0 + n]
+        def cast(on_vector, chunk, lo, hi):
+            a, j0, nj, r0, n = CHUNKS[chunk]
             (p0, piece), = [(t0, g[a][i]) for i, (t0, n) in enumerate(PIECES[a]) if t0 <= lo < t0 + n]
-            weave(on_vector, piece[:, lo - p0 : hi - p0, :], raw[:, :, lo - r0 : hi - r0])
+            to = piece[:, lo - p0 : hi - p0, j0 : j0 + nj]
+            rows = raws[chunk][:, :, lo - r0 : hi - r0]
+            if nj == 4:
+                to = to.rearrange("p (c i) j -> p c j i", i=4)
+                rows = rows.rearrange("p j (c i) -> p c j i", i=4)
+            else:
+                rows = rows.rearrange("p j t -> p t j")
+            if on_vector:
+                nc.vector.tensor_copy(to, rows)
+            else:
+                nc.scalar.activation(to, rows, COPY)
 
         def quantize(a, i):
             t0, n = PIECES[a][i]
@@ -114,23 +114,22 @@ def tile_moe_two_lin_gelu_kernel(tc, xT, w_words, w_scales, b, gate, offs, dst, 
         def gather_bytes(h):
             nc.vector.tensor_copy(gb[h][:], xs[:].indirect(list_of(offs_t, h)))
 
-        cast(True, 0, 0, 256)
-        cast(False, 0, 256, 384)
+        for pair in range(2):
+            cast(True, pair, 0, 256)
+            cast(True, pair, 256, 320)
+            cast(False, pair, 320, 512)
+            cast(False, pair, 512, 640)
         gate_t = keep.tile([P, S], F32, name="gate_t", tag="raw0")
         nc.sync.dma_start(gate_t[:], gate)
-        quantize(0, 0)
-        quantize(0, 1)
-        cast(True, 0, 384, 544)
-        cast(False, 0, 544, 640)
-        quantize(0, 2)
-        cast(False, 1, 0, 256)
+        for i in range(3):
+            quantize(0, i)
+        cast(False, 2, 0, 256)
         nc.vector.tensor_copy(gw0[:], xw[0][:].indirect(offs_t[:]))
         quantize(1, 0)
-        cast(True, 1, 256, 320)
-        cast(False, 1, 320, 448)
-        cast(True, 1, 448, 512)
-        cast(True, 1, 512, 576)
-        cast(False, 1, 576, 640)
+        cast(False, 3, 256, 448)
+        cast(True, 4, 448, 512)
+        cast(True, 4, 512, 576)
+        cast(False, 4, 576, 640)
         quantize(1, 1)
         quantize(1, 2)
 

@@ -18,7 +18,7 @@ GELU = mybir.ActivationFunctionType.Gelu_apprx_tanh
 COPY = mybir.ActivationFunctionType.Copy
 MULT = mybir.AluOpType.mult
 
-CHUNKS = ((0, 0, 2, 0, 640), (0, 2, 2, 0, 640), (1, 0, 4, 0, 256), (1, 0, 4, 256, 192), (1, 0, 4, 448, 192))
+CHUNKS = ((0, 0, 2, 0, 640), (0, 2, 2, 0, 640), (1, 0, 4, 0, 256), (1, 0, 4, 256, 256), (1, 0, 4, 512, 128))
 PIECES = (((0, 256), (256, 256), (512, 128)), ((0, 256), (256, 256), (512, 128)))
 WINDOW = 704
 
@@ -126,8 +126,8 @@ def tile_moe_two_lin_gelu_kernel(tc, xT, w_words, w_scales, b, gate, offs, dst, 
         cast(False, 2, 0, 256)
         nc.vector.tensor_copy(gw0[:], xw[0][:].indirect(offs_t[:]))
         quantize(1, 0)
-        cast(False, 3, 256, 448)
-        cast(True, 4, 448, 512)
+        cast(True, 3, 256, 368)
+        cast(False, 3, 368, 512)
         cast(True, 4, 512, 576)
         cast(False, 4, 576, 640)
         quantize(1, 1)

@@ -20,7 +20,6 @@ MULT = mybir.AluOpType.mult
 
 CHUNKS = ((0, 0, 2, 0, 640), (0, 2, 2, 0, 640), (1, 0, 4, 0, 256), (1, 0, 4, 256, 256), (1, 0, 4, 512, 128))
 PIECES = (((0, 256), (256, 256), (512, 128)), ((0, 256), (256, 256), (512, 128)))
-WINDOW = 704
 
 
 def tile_moe_two_lin_gelu_kernel(tc, xT, w_words, w_scales, b, gate, offs, dst, out):
@@ -61,24 +60,23 @@ def tile_moe_two_lin_gelu_kernel(tc, xT, w_words, w_scales, b, gate, offs, dst, 
             return w_t
 
         ww = [load_words(0)]
-        for q in range(4):
+        for r in range(4):
             nc.sync.dma_start(
-                ws[32 * q : 32 * q + 4, :, :].bitcast(I32),
-                w_scales[:, :, 4 * q : 4 * q + 4, :].rearrange("e a q n -> q (e a) n").bitcast(I32),
+                ws[r:P:32, :, :].bitcast(I32),
+                w_scales[:, :, r:16:4, :].rearrange("e a q n -> q (e a) n").bitcast(I32),
             )
         nc.sync.dma_start(b_t[:], b)
         ww.append(load_words(1))
         nc.sync.dma_start(dst_t[:], dst)
 
-        xw = [keep.tile([P, n], U32, name=f"xw{a}", align_bytes=64) for a, n in enumerate((WINDOW, T))]
-        nc.vector.memset(xw[0][:, T:WINDOW].bitcast(I32), 0)
-        gw0 = keep.tile([P, S], U32, name="gw0", align_bytes=64)
+        xw = [keep.tile([P, T], U32, name=f"xw{a}", align_bytes=64) for a in range(2)]
+        gw0 = keep.tile([P, 3 * C], U32, name="gw0", align_bytes=64)
         gw1 = [keep.tile([P, 2 * C], U32, name=f"gw1{h}", align_bytes=64) for h in range(2)]
-        gw = [[gw0[:, 0 : 2 * C], gw0[:, 2 * C : S]], [gw1[0][:], gw1[1][:]]]
+        gw = [None, [gw1[0][:], gw1[1][:]]]
         gb = [keep.tile([P, 2 * C], U8, name=f"gb{h}", align_bytes=64) for h in range(2)]
 
         g = [
-            [keep.tile([P, n, 4], BF16, name=f"g{a}{i}", align_bytes=64) for i, (t0, n) in enumerate(PIECES[a])]
+            [keep.tile([P, n, 4], BF16, name=f"g{a}{i}", tag=f"g{a}{i}", align_bytes=64) for i, (t0, n) in enumerate(PIECES[a])]
             for a in range(2)
         ]
 
@@ -124,7 +122,7 @@ def tile_moe_two_lin_gelu_kernel(tc, xT, w_words, w_scales, b, gate, offs, dst, 
         for i in range(3):
             quantize(0, i)
         cast(False, 2, 0, 256)
-        nc.vector.tensor_copy(gw0[:], xw[0][:].indirect(offs_t[:]))
+        nc.vector.tensor_copy(gw0[:], xw[0][:].indirect(offs_t[:, 0:24]))
         quantize(1, 0)
         cast(True, 3, 256, 368)
         cast(False, 3, 368, 512)
@@ -132,13 +130,20 @@ def tile_moe_two_lin_gelu_kernel(tc, xT, w_words, w_scales, b, gate, offs, dst, 
         cast(False, 4, 576, 640)
         quantize(1, 1)
         quantize(1, 2)
+        gw03 = keep.tile([P, C], U32, name="gw03", tag="g11", align_bytes=64)
+        nc.vector.tensor_copy(gw03[:], xw[0][:].indirect(offs_t[:, 24:32]))
+        first = [gw0[:, 0:C], gw0[:, C : 2 * C], gw0[:, 2 * C : 3 * C], gw03[:]]
 
         ys = []
         for h in range(2):
             y = keep.tile([P, 2 * C], F32, name=f"y{h}")
             ys.append(y)
             gather_bytes(h)
-            gather_words(1, h)
+            if h == 0:
+                for e in range(2):
+                    nc.vector.tensor_copy(gw[1][0][:, e * C : (e + 1) * C], xw[1][:].indirect(offs_t[:, 8 * e : 8 * e + 8]))
+            else:
+                gather_words(1, h)
             ps = [psum.tile([P, C], F32, name=f"ps{2 * h + i}") for i in range(2)]
             for a in range(2):
                 for i in range(2):
@@ -147,7 +152,7 @@ def tile_moe_two_lin_gelu_kernel(tc, xT, w_words, w_scales, b, gate, offs, dst, 
                         out=ps[i][:],
                         lhsT=ww[h][:, 2 * i + a, :].bitcast(FP8X4),
                         lhsT_scale=ws[:, 2 * (2 * h + i) + a, :],
-                        rhs=gw[a][h][:, c].bitcast(FP8X4),
+                        rhs=(gw[1][h][:, c] if a else first[2 * h + i]).bitcast(FP8X4),
                         rhs_scale=gb[h][4 * a : P, c],
                         start=(a == 0),
                         stop=(a == 1),

@@ -66,8 +66,10 @@ def tile_moe_two_lin_gelu_kernel(tc, xT, w_words, w_scales, b, gate, offs, dst, 
                 w_scales[:, :, r:16:4, :].rearrange("e a q n -> q (e a) n").bitcast(I32),
             )
         nc.sync.dma_start(b_t[:], b)
-        ww.append(load_words(1))
+        gate_t = keep.tile([P, S], F32, name="gate_t")
+        nc.sync.dma_start(gate_t[:], gate)
         nc.sync.dma_start(dst_t[:], dst)
+        ww.append(load_words(1))
 
         xw = [keep.tile([P, T], U32, name=f"xw{a}", align_bytes=64) for a in range(2)]
         gw0 = keep.tile([P, 3 * C], U32, name="gw0", align_bytes=64)
@@ -117,8 +119,6 @@ def tile_moe_two_lin_gelu_kernel(tc, xT, w_words, w_scales, b, gate, offs, dst, 
             cast(True, pair, 256, 320)
             cast(False, pair, 320, 512)
             cast(False, pair, 512, 640)
-        gate_t = keep.tile([P, S], F32, name="gate_t", tag="raw0")
-        nc.sync.dma_start(gate_t[:], gate)
         for i in range(3):
             quantize(0, i)
         cast(False, 2, 0, 256)

@@ -123,6 +123,8 @@ def tile_moe_two_lin_gelu_kernel(tc, xT, w_words, w_scales, b, gate, offs, dst, 
             quantize(0, i)
         cast(False, 2, 0, 256)
         nc.vector.tensor_copy(gw0[:], xw[0][:].indirect(offs_t[:, 0:24]))
+        gw03 = keep.tile([P, C], U32, name="gw03", align_bytes=64)
+        nc.vector.tensor_copy(gw03[:], xw[0][:].indirect(offs_t[:, 24:32]))
         quantize(1, 0)
         cast(True, 3, 256, 368)
         cast(False, 3, 368, 512)
@@ -130,8 +132,6 @@ def tile_moe_two_lin_gelu_kernel(tc, xT, w_words, w_scales, b, gate, offs, dst, 
         cast(False, 4, 576, 640)
         quantize(1, 1)
         quantize(1, 2)
-        gw03 = keep.tile([P, C], U32, name="gw03", tag="g11", align_bytes=64)
-        nc.vector.tensor_copy(gw03[:], xw[0][:].indirect(offs_t[:, 24:32]))
         first = [gw0[:, 0:C], gw0[:, C : 2 * C], gw0[:, 2 * C : 3 * C], gw03[:]]
 
         ys = []

@@ -18,8 +18,16 @@ GELU = mybir.ActivationFunctionType.Gelu_apprx_tanh
 COPY = mybir.ActivationFunctionType.Copy
 MULT = mybir.AluOpType.mult
 
-CHUNKS = ((0, 0, 2, 0, 640), (0, 2, 2, 0, 640), (1, 0, 4, 0, 256), (1, 0, 4, 256, 256), (1, 0, 4, 512, 128))
-PIECES = (((0, 256), (256, 256), (512, 128)), ((0, 256), (256, 256), (512, 128)))
+PASSES = 2
+ROWS = 4
+HALVES = 2
+HALF = S // HALVES
+PER_COLUMN = 16
+SCALE_ROWS = 4
+
+PIECES = ((0, 256), (256, 256), (512, 128))
+LOADS = ((0, 0, 2, 0, T), (0, 2, 2, 0, T)) + tuple((1, 0, ROWS, t0, n) for t0, n in PIECES)
+VECTOR_SHARE = ((256, 64, 0), (0, 112, 64))
 
 
 def tile_moe_two_lin_gelu_kernel(tc, xT, w_words, w_scales, b, gate, offs, dst, out):
@@ -28,144 +36,143 @@ def tile_moe_two_lin_gelu_kernel(tc, xT, w_words, w_scales, b, gate, offs, dst, 
         keep = ctx.enter_context(tc.tile_pool(name="keep", bufs=1))
         psum = ctx.enter_context(tc.psum_pool(name="psum", bufs=1))
 
-        offs_t = keep.tile([P, S // 16], U16, name="offs_t")
-        dst_t = keep.tile([P, S // 16], U16, name="dst_t")
+        offs_t = keep.tile([P, S // PER_COLUMN], U16, name="offs_t")
+        dst_t = keep.tile([P, S // PER_COLUMN], U16, name="dst_t")
         b_t = keep.tile([P, E], F32, name="b_t")
 
         raws = []
-        for i, (a, j0, nj, t0, n) in enumerate(CHUNKS):
-            raw = keep.tile([P, nj, n], F32, name=f"raw{i}", tag=f"raw{i}")
-            rows = xT[512 * a : 512 * (a + 1), t0 : t0 + n].rearrange("(p j) t -> p j t", j=4)
-            nc.sync.dma_start(raw[:], rows[:, j0 : j0 + nj, :])
-            raws.append(raw)
-            if i == 1:
-                nc.sync.dma_start(offs_t[:], offs)
 
-        ws = keep.tile([P, 2 * E, N], U8, name="ws", align_bytes=64)
-        nc.vector.memset(ws[:].rearrange("p g n -> p (g n)").bitcast(I32), 0)
-        xs = keep.tile([P, T], U8, name="xs", align_bytes=64)
-        nc.gpsimd.memset(xs[:].bitcast(I32), 0)
-        o_t = keep.tile([P, T], F32, name="o_t")
-        nc.vector.memset(o_t[:], 0.0)
+        def load_x(a, r0, rows, t0, n):
+            raw = keep.tile([P, rows, n], F32, name=f"raw{len(raws)}")
+            by_row = xT[P * ROWS * a : P * ROWS * (a + 1), t0 : t0 + n].rearrange("(p r) t -> p r t", r=ROWS)
+            nc.sync.dma_start(raw[:], by_row[:, r0 : r0 + rows, :])
+            raws.append(raw)
+
+        for load in LOADS[:2]:
+            load_x(*load)
+        nc.sync.dma_start(offs_t[:], offs)
+        for load in LOADS[2:]:
+            load_x(*load)
+
+        w_scale_t = keep.tile([P, PASSES * E, N], U8, name="w_scale_t", align_bytes=64)
+        nc.vector.memset(w_scale_t[:].rearrange("p g n -> p (g n)").bitcast(I32), 0)
+        x_scale_t = keep.tile([P, T], U8, name="x_scale_t", align_bytes=64)
+        nc.gpsimd.memset(x_scale_t[:].bitcast(I32), 0)
+        out_t = keep.tile([P, T], F32, name="out_t")
+        nc.vector.memset(out_t[:], 0.0)
         warm = keep.tile([P, 1], F32, name="warm")
         nc.vector.memset(warm[:], 0.0)
         nc.scalar.activation(warm[:], warm[:], GELU)
 
-        def load_words(h):
-            w_t = keep.tile([P, 4, N], I32, name=f"w{h}", align_bytes=64)
+        def load_w_words(h):
+            words = keep.tile([P, PASSES * E // HALVES, N], I32, name=f"w_words{h}", align_bytes=64)
             nc.sync.dma_start(
-                w_t[:],
+                words[:],
                 w_words[2 * h : 2 * h + 2].rearrange("e a p n r -> p (e a) (n r)").bitcast(I32),
             )
-            return w_t
+            return words
 
-        ww = [load_words(0)]
-        for r in range(4):
+        w_words_t = [load_w_words(0)]
+        for s0 in range(SCALE_ROWS):
             nc.sync.dma_start(
-                ws[r:P:32, :, :].bitcast(I32),
-                w_scales[:, :, r:16:4, :].rearrange("e a q n -> q (e a) n").bitcast(I32),
+                w_scale_t[s0:P:32, :, :].bitcast(I32),
+                w_scales[:, :, s0:16:SCALE_ROWS, :].rearrange("e a s n -> s (e a) n").bitcast(I32),
             )
         nc.sync.dma_start(b_t[:], b)
         gate_t = keep.tile([P, S], F32, name="gate_t")
         nc.sync.dma_start(gate_t[:], gate)
         nc.sync.dma_start(dst_t[:], dst)
-        ww.append(load_words(1))
+        w_words_t.append(load_w_words(1))
 
-        xw = [keep.tile([P, T], U32, name=f"xw{a}", align_bytes=64) for a in range(2)]
-        gw0 = keep.tile([P, 3 * C], U32, name="gw0", align_bytes=64)
-        gw1 = [keep.tile([P, 2 * C], U32, name=f"gw1{h}", align_bytes=64) for h in range(2)]
-        gw = [None, [gw1[0][:], gw1[1][:]]]
-        gb = [keep.tile([P, 2 * C], U8, name=f"gb{h}", align_bytes=64) for h in range(2)]
-
-        g = [
-            [keep.tile([P, n, 4], BF16, name=f"g{a}{i}", tag=f"g{a}{i}", align_bytes=64) for i, (t0, n) in enumerate(PIECES[a])]
-            for a in range(2)
+        token_words = [keep.tile([P, T], U32, name=f"token_words{a}", align_bytes=64) for a in range(PASSES)]
+        slot_words = [
+            [keep.tile([P, HALF], U32, name=f"slot_words{a}{h}", align_bytes=64) for h in range(HALVES)]
+            for a in range(PASSES)
+        ]
+        slot_scales = [keep.tile([P, HALF], U8, name=f"slot_scales{h}", align_bytes=64) for h in range(HALVES)]
+        rounded = [
+            [keep.tile([P, n, ROWS], BF16, name=f"rounded{a}{i}", align_bytes=64) for i, (t0, n) in enumerate(PIECES)]
+            for a in range(PASSES)
         ]
 
-        def cast(on_vector, chunk, lo, hi):
-            a, j0, nj, r0, n = CHUNKS[chunk]
-            (p0, piece), = [(t0, g[a][i]) for i, (t0, n) in enumerate(PIECES[a]) if t0 <= lo < t0 + n]
-            to = piece[:, lo - p0 : hi - p0, j0 : j0 + nj]
-            rows = raws[chunk][:, :, lo - r0 : hi - r0]
-            if nj == 4:
-                to = to.rearrange("p (c i) j -> p c j i", i=4)
-                rows = rows.rearrange("p j (c i) -> p c j i", i=4)
-            else:
-                rows = rows.rearrange("p j t -> p t j")
-            if on_vector:
-                nc.vector.tensor_copy(to, rows)
-            else:
-                nc.scalar.activation(to, rows, COPY)
+        def cast(load, i):
+            a, r0, rows, raw_t0, raw_n = LOADS[load]
+            t0, n = PIECES[i]
+            share = VECTOR_SHARE[a][i]
+            for on_vector, lo, hi in ((True, 0, share), (False, share, n)):
+                if lo == hi:
+                    continue
+                target = rounded[a][i][:, lo:hi, r0 : r0 + rows]
+                source = raws[load][:, :, t0 - raw_t0 + lo : t0 - raw_t0 + hi]
+                if rows == ROWS:
+                    target = target.rearrange("p (c u) r -> p c r u", u=4)
+                    source = source.rearrange("p r (c u) -> p c r u", u=4)
+                else:
+                    source = source.rearrange("p r t -> p t r")
+                if on_vector:
+                    nc.vector.tensor_copy(target, source)
+                else:
+                    nc.scalar.activation(target, source, COPY)
 
         def quantize(a, i):
-            t0, n = PIECES[a][i]
+            t0, n = PIECES[i]
             nc.vector.quantize_mx(
-                out=xw[a][:, t0 : t0 + n].bitcast(FP8X4),
-                scales=xs[4 * a : P, t0 : t0 + n],
-                in_=g[a][i][:].rearrange("p t j -> p (t j)"),
+                out=token_words[a][:, t0 : t0 + n].bitcast(FP8X4),
+                scales=x_scale_t[SCALE_ROWS * a : P, t0 : t0 + n],
+                in_=rounded[a][i][:].rearrange("p t r -> p (t r)"),
             )
 
-        def list_of(tile, h):
-            return tile[:, 16 * h : 16 * h + 16]
+        def entries(list_t, j0, n):
+            return list_t[:, j0 // PER_COLUMN : (j0 + n) // PER_COLUMN]
 
-        def gather_words(a, h):
-            nc.vector.tensor_copy(gw[a][h], xw[a][:].indirect(list_of(offs_t, h)))
+        def gather_words(a, j0, n):
+            h, c0 = divmod(j0, HALF)
+            nc.vector.tensor_copy(slot_words[a][h][:, c0 : c0 + n], token_words[a][:].indirect(entries(offs_t, j0, n)))
 
-        def gather_bytes(h):
-            nc.vector.tensor_copy(gb[h][:], xs[:].indirect(list_of(offs_t, h)))
-
-        for pair in range(2):
-            cast(True, pair, 0, 256)
-            cast(True, pair, 256, 320)
-            cast(False, pair, 320, 512)
-            cast(False, pair, 512, 640)
-        for i in range(3):
+        for load in range(2):
+            for i in range(len(PIECES)):
+                cast(load, i)
+        for i in range(len(PIECES)):
             quantize(0, i)
-        cast(False, 2, 0, 256)
-        nc.vector.tensor_copy(gw0[:], xw[0][:].indirect(offs_t[:, 0:24]))
-        gw03 = keep.tile([P, C], U32, name="gw03", align_bytes=64)
-        nc.vector.tensor_copy(gw03[:], xw[0][:].indirect(offs_t[:, 24:32]))
+        cast(2, 0)
+        for h in range(HALVES):
+            gather_words(0, h * HALF, HALF)
         quantize(1, 0)
-        cast(True, 3, 256, 368)
-        cast(False, 3, 368, 512)
-        cast(True, 4, 512, 576)
-        cast(False, 4, 576, 640)
+        cast(3, 1)
+        cast(4, 2)
         quantize(1, 1)
         quantize(1, 2)
-        first = [gw0[:, 0:C], gw0[:, C : 2 * C], gw0[:, 2 * C : 3 * C], gw03[:]]
 
-        ys = []
-        for h in range(2):
-            y = keep.tile([P, 2 * C], F32, name=f"y{h}")
-            ys.append(y)
-            gather_bytes(h)
-            if h == 0:
-                for e in range(2):
-                    nc.vector.tensor_copy(gw[1][0][:, e * C : (e + 1) * C], xw[1][:].indirect(offs_t[:, 8 * e : 8 * e + 8]))
-            else:
-                gather_words(1, h)
-            ps = [psum.tile([P, C], F32, name=f"ps{2 * h + i}") for i in range(2)]
-            for a in range(2):
+        acts = []
+        for h in range(HALVES):
+            act = keep.tile([P, HALF], F32, name=f"act{h}")
+            acts.append(act)
+            nc.vector.tensor_copy(slot_scales[h][:], x_scale_t[:].indirect(entries(offs_t, h * HALF, HALF)))
+            step = C if h == 0 else HALF
+            for j0 in range(h * HALF, (h + 1) * HALF, step):
+                gather_words(1, j0, step)
+            sums = [psum.tile([P, C], F32, name=f"sums{2 * h + i}") for i in range(2)]
+            for a in range(PASSES):
                 for i in range(2):
-                    c = slice(i * C, (i + 1) * C)
+                    cols = slice(i * C, (i + 1) * C)
                     nc.tensor.matmul_mx(
-                        out=ps[i][:],
-                        lhsT=ww[h][:, 2 * i + a, :].bitcast(FP8X4),
-                        lhsT_scale=ws[:, 2 * (2 * h + i) + a, :],
-                        rhs=(gw[1][h][:, c] if a else first[2 * h + i]).bitcast(FP8X4),
-                        rhs_scale=gb[h][4 * a : P, c],
+                        out=sums[i][:],
+                        lhsT=w_words_t[h][:, PASSES * i + a, :].bitcast(FP8X4),
+                        lhsT_scale=w_scale_t[:, PASSES * (2 * h + i) + a, :],
+                        rhs=slot_words[a][h][:, cols].bitcast(FP8X4),
+                        rhs_scale=slot_scales[h][SCALE_ROWS * a : P, cols],
                         start=(a == 0),
-                        stop=(a == 1),
+                        stop=(a == PASSES - 1),
                     )
             for i in range(2):
                 e = 2 * h + i
-                nc.scalar.activation(y[:, i * C : (i + 1) * C], ps[i][:], GELU, bias=b_t[:, e : e + 1])
+                nc.scalar.activation(act[:, i * C : (i + 1) * C], sums[i][:], GELU, bias=b_t[:, e : e + 1])
 
-        for h in range(2):
+        for h in range(HALVES):
             nc.vector.tensor_tensor(
-                o_t[:].indirect(list_of(dst_t, h)),
-                ys[h][:],
-                gate_t[:, 2 * h * C : 2 * (h + 1) * C],
+                out_t[:].indirect(entries(dst_t, h * HALF, HALF)),
+                acts[h][:],
+                gate_t[:, h * HALF : (h + 1) * HALF],
                 MULT,
             )
-        nc.sync.dma_start(out, o_t[:])
+        nc.sync.dma_start(out, out_t[:])

@@ -51,13 +51,15 @@ def tile_moe_two_lin_gelu_kernel(tc, xT, w_words, w_scales, b, gate, offs, dst, 
         for load in LOADS[:2]:
             load_x(*load)
         nc.sync.dma_start(offs_t[:], offs)
-        for load in LOADS[2:]:
-            load_x(*load)
+        raw1 = keep.tile([P, ROWS, T], F32, name="raw_pass1")
+        by_row1 = xT[P * ROWS : 2 * P * ROWS, :].rearrange("(p r) t -> p r t", r=ROWS)
+        for t0, n in PIECES:
+            nc.sync.dma_start(raw1[:, :, t0 : t0 + n], by_row1[:, :, t0 : t0 + n])
 
         w_scale_t = keep.tile([P, PASSES * E, N], U8, name="w_scale_t", align_bytes=64)
         nc.vector.memset(w_scale_t[:].rearrange("p g n -> p (g n)").bitcast(I32), 0)
         x_scale_t = keep.tile([P, T], U8, name="x_scale_t", align_bytes=64)
-        nc.gpsimd.memset(x_scale_t[:].bitcast(I32), 0)
+        nc.vector.memset(x_scale_t[:].bitcast(I32), 0)
         out_t = keep.tile([P, T], F32, name="out_t")
         nc.vector.memset(out_t[:], 0.0)
         warm = keep.tile([P, 1], F32, name="warm")
@@ -92,8 +94,18 @@ def tile_moe_two_lin_gelu_kernel(tc, xT, w_words, w_scales, b, gate, offs, dst, 
         slot_scales = [keep.tile([P, HALF], U8, name=f"slot_scales{h}", align_bytes=64) for h in range(HALVES)]
         rounded = [
             [keep.tile([P, n, ROWS], BF16, name=f"rounded{a}{i}", align_bytes=64) for i, (t0, n) in enumerate(PIECES)]
-            for a in range(PASSES)
+            for a in range(1)
         ]
+
+        rounded1 = keep.tile([P, T, ROWS], BF16, name="rounded1", align_bytes=64)
+
+        def cast1(on_vector, lo, hi):
+            target = rounded1[:, lo:hi, :].rearrange("p (c u) r -> p c r u", u=4)
+            source = raw1[:, :, lo:hi].rearrange("p r (c u) -> p c r u", u=4)
+            if on_vector:
+                nc.vector.tensor_copy(target, source)
+            else:
+                nc.scalar.activation(target, source, COPY)
 
         def cast(load, i):
             a, r0, rows, raw_t0, raw_n = LOADS[load]
@@ -119,7 +131,7 @@ def tile_moe_two_lin_gelu_kernel(tc, xT, w_words, w_scales, b, gate, offs, dst, 
             nc.vector.quantize_mx(
                 out=token_words[a][:, t0 : t0 + n].bitcast(FP8X4),
                 scales=x_scale_t[SCALE_ROWS * a : P, t0 : t0 + n],
-                in_=rounded[a][i][:].rearrange("p t r -> p (t r)"),
+                in_=(rounded[0][i][:] if a == 0 else rounded1[:, t0 : t0 + n, :]).rearrange("p t r -> p (t r)"),
             )
 
         def entries(list_t, j0, n):
@@ -134,12 +146,15 @@ def tile_moe_two_lin_gelu_kernel(tc, xT, w_words, w_scales, b, gate, offs, dst, 
                 cast(load, i)
         for i in range(len(PIECES)):
             quantize(0, i)
-        cast(2, 0)
+        cast1(False, 0, 240)
         for h in range(HALVES):
             gather_words(0, h * HALF, HALF)
+        cast1(True, 384, 512)
+        cast1(False, 240, 272)
+        cast1(False, 272, 384)
         quantize(1, 0)
-        cast(3, 1)
-        cast(4, 2)
+        cast1(True, 512, 576)
+        cast1(False, 576, 640)
         quantize(1, 1)
         quantize(1, 2)
 

@@ -19,6 +19,7 @@ COPY = mybir.ActivationFunctionType.Copy
 MULT = mybir.AluOpType.mult
 
 PASSES = 2
+TAIL = 8
 ROWS = 4
 HALVES = 2
 HALF = S // HALVES
@@ -181,9 +182,14 @@ def tile_moe_two_lin_gelu_kernel(tc, xT, w_words, w_scales, b, gate, offs, dst, 
                     )
             for i in range(2):
                 e = 2 * h + i
-                nc.scalar.activation(act[:, i * C : (i + 1) * C], sums[i][:], GELU, bias=b_t[:, e : e + 1])
+                n = C - TAIL if e == E - 1 else C
+                nc.scalar.activation(act[:, i * C : i * C + n], sums[i][:, :n], GELU, bias=b_t[:, e : e + 1])
+        tail = keep.tile([P, TAIL], F32, name="tail")
+        nc.scalar.activation(tail[:], sums[1][:, C - TAIL :], GELU, bias=b_t[:, E - 1 : E])
 
         for h in range(HALVES):
+            if h == 1:
+                nc.vector.tensor_copy(acts[1][:, HALF - TAIL :], tail[:])
             nc.vector.tensor_tensor(
                 out_t[:].indirect(entries(dst_t, h * HALF, HALF)),
                 acts[h][:],

@@ -19,16 +19,18 @@ COPY = mybir.ActivationFunctionType.Copy
 MULT = mybir.AluOpType.mult
 
 PASSES = 2
-TAIL = 8
 ROWS = 4
+PAIR = 2
 HALVES = 2
 HALF = S // HALVES
 PER_COLUMN = 16
 SCALE_ROWS = 4
 
-PIECES = ((0, 256), (256, 256), (512, 128))
-LOADS = ((0, 0, 2, 0, T), (0, 2, 2, 0, T)) + tuple((1, 0, ROWS, t0, n) for t0, n in PIECES)
-VECTOR_SHARE = ((256, 64, 0), (0, 112, 64))
+PIECES = ((0, 256), (256, 512), (512, 640))
+PASS0_VECTOR = (256, 64, 0)
+PASS1_VECTOR = (0, 128, 48)
+BRIDGE = 8
+TAIL = 8
 
 
 def tile_moe_two_lin_gelu_kernel(tc, xT, w_words, w_scales, b, gate, offs, dst, out):
@@ -41,21 +43,16 @@ def tile_moe_two_lin_gelu_kernel(tc, xT, w_words, w_scales, b, gate, offs, dst, 
         dst_t = keep.tile([P, S // PER_COLUMN], U16, name="dst_t")
         b_t = keep.tile([P, E], F32, name="b_t")
 
-        raws = []
-
-        def load_x(a, r0, rows, t0, n):
-            raw = keep.tile([P, rows, n], F32, name=f"raw{len(raws)}")
-            by_row = xT[P * ROWS * a : P * ROWS * (a + 1), t0 : t0 + n].rearrange("(p r) t -> p r t", r=ROWS)
-            nc.sync.dma_start(raw[:], by_row[:, r0 : r0 + rows, :])
-            raws.append(raw)
-
-        for load in LOADS[:2]:
-            load_x(*load)
+        x_rows = xT.rearrange("(a p r) t -> a p r t", a=PASSES, r=ROWS)
+        raw_pairs = []
+        for r0 in range(0, ROWS, PAIR):
+            raw_pair = keep.tile([P, PAIR, T], F32, name=f"raw_pair{r0}")
+            nc.sync.dma_start(raw_pair[:], x_rows[0, :, r0 : r0 + PAIR, :])
+            raw_pairs.append(raw_pair)
         nc.sync.dma_start(offs_t[:], offs)
-        raw1 = keep.tile([P, ROWS, T], F32, name="raw_pass1")
-        by_row1 = xT[P * ROWS : 2 * P * ROWS, :].rearrange("(p r) t -> p r t", r=ROWS)
-        for t0, n in PIECES:
-            nc.sync.dma_start(raw1[:, :, t0 : t0 + n], by_row1[:, :, t0 : t0 + n])
+        raw_pass1 = keep.tile([P, ROWS, T], F32, name="raw_pass1")
+        for t0, t1 in PIECES:
+            nc.sync.dma_start(raw_pass1[:, :, t0:t1], x_rows[1, :, :, t0:t1])
 
         w_scale_t = keep.tile([P, PASSES * E, N], U8, name="w_scale_t", align_bytes=64)
         nc.vector.memset(w_scale_t[:].rearrange("p g n -> p (g n)").bitcast(I32), 0)
@@ -93,46 +90,31 @@ def tile_moe_two_lin_gelu_kernel(tc, xT, w_words, w_scales, b, gate, offs, dst, 
             for a in range(PASSES)
         ]
         slot_scales = [keep.tile([P, HALF], U8, name=f"slot_scales{h}", align_bytes=64) for h in range(HALVES)]
-        rounded = [
-            [keep.tile([P, n, ROWS], BF16, name=f"rounded{a}{i}", align_bytes=64) for i, (t0, n) in enumerate(PIECES)]
-            for a in range(1)
-        ]
+        rounded = [keep.tile([P, T, ROWS], BF16, name=f"rounded{a}", align_bytes=64) for a in range(PASSES)]
 
-        rounded1 = keep.tile([P, T, ROWS], BF16, name="rounded1", align_bytes=64)
-
-        def cast1(on_vector, lo, hi):
-            target = rounded1[:, lo:hi, :].rearrange("p (c u) r -> p c r u", u=4)
-            source = raw1[:, :, lo:hi].rearrange("p r (c u) -> p c r u", u=4)
+        def cast(on_vector, target, source):
             if on_vector:
                 nc.vector.tensor_copy(target, source)
             else:
                 nc.scalar.activation(target, source, COPY)
 
-        def cast(load, i):
-            a, r0, rows, raw_t0, raw_n = LOADS[load]
-            t0, n = PIECES[i]
-            share = VECTOR_SHARE[a][i]
-            for on_vector, lo, hi in ((True, 0, share), (False, share, n)):
-                if lo == hi:
-                    continue
-                target = rounded[a][i][:, lo:hi, r0 : r0 + rows]
-                source = raws[load][:, :, t0 - raw_t0 + lo : t0 - raw_t0 + hi]
-                if rows == ROWS:
-                    target = target.rearrange("p (c u) r -> p c r u", u=4)
-                    source = source.rearrange("p r (c u) -> p c r u", u=4)
-                else:
-                    source = source.rearrange("p r t -> p t r")
-                if on_vector:
-                    nc.vector.tensor_copy(target, source)
-                else:
-                    nc.scalar.activation(target, source, COPY)
+        def cast_pair(on_vector, pair, t0, t1):
+            rows = slice(PAIR * pair, PAIR * (pair + 1))
+            cast(on_vector, rounded[0][:, t0:t1, rows], raw_pairs[pair][:, :, t0:t1].rearrange("p r t -> p t r"))
 
-        def quantize(a, i):
-            t0, n = PIECES[i]
+        def cast_pass1(on_vector, t0, t1):
+            cast(
+                on_vector,
+                rounded[1][:, t0:t1, :].rearrange("p (c u) r -> p c r u", u=4),
+                raw_pass1[:, :, t0:t1].rearrange("p r (c u) -> p c r u", u=4),
+            )
+
+        def quantize(a, piece):
+            t0, t1 = PIECES[piece]
             nc.vector.quantize_mx(
-                out=token_words[a][:, t0 : t0 + n].bitcast(FP8X4),
-                scales=x_scale_t[SCALE_ROWS * a : P, t0 : t0 + n],
-                in_=(rounded[0][i][:] if a == 0 else rounded1[:, t0 : t0 + n, :]).rearrange("p t r -> p (t r)"),
+                out=token_words[a][:, t0:t1].bitcast(FP8X4),
+                scales=x_scale_t[SCALE_ROWS * a : P, t0:t1],
+                in_=rounded[a][:, t0:t1, :].rearrange("p t r -> p (t r)"),
             )
 
         def entries(list_t, j0, n):
@@ -142,27 +124,31 @@ def tile_moe_two_lin_gelu_kernel(tc, xT, w_words, w_scales, b, gate, offs, dst, 
             h, c0 = divmod(j0, HALF)
             nc.vector.tensor_copy(slot_words[a][h][:, c0 : c0 + n], token_words[a][:].indirect(entries(offs_t, j0, n)))
 
-        for load in range(2):
-            for i in range(len(PIECES)):
-                cast(load, i)
-        for i in range(len(PIECES)):
-            quantize(0, i)
-        cast1(False, 0, 240)
+        for pair in range(ROWS // PAIR):
+            for (t0, t1), share in zip(PIECES, PASS0_VECTOR):
+                if share > 0:
+                    cast_pair(True, pair, t0, t0 + share)
+                if t0 + share < t1:
+                    cast_pair(False, pair, t0 + share, t1)
+        for piece in range(len(PIECES)):
+            quantize(0, piece)
+        first_border, second_border = PIECES[1]
+        cast_pass1(False, 0, first_border - BRIDGE)
         for h in range(HALVES):
             gather_words(0, h * HALF, HALF)
-        cast1(True, 384, 512)
-        cast1(False, 240, 272)
-        cast1(False, 272, 384)
+
+        cast_pass1(True, second_border - PASS1_VECTOR[1], second_border)
+        cast_pass1(False, first_border - BRIDGE, first_border + BRIDGE)
+        cast_pass1(False, first_border + BRIDGE, second_border - PASS1_VECTOR[1])
         quantize(1, 0)
-        cast1(True, 512, 576)
-        cast1(False, 576, 640)
+        cast_pass1(True, second_border, second_border + PASS1_VECTOR[2])
+        cast_pass1(False, second_border + PASS1_VECTOR[2], T)
         quantize(1, 1)
         quantize(1, 2)
 
-        acts = []
+        acts = [keep.tile([P, HALF], F32, name=f"act{h}") for h in range(HALVES)]
+        act_tail = keep.tile([P, TAIL], F32, name="act_tail")
         for h in range(HALVES):
-            act = keep.tile([P, HALF], F32, name=f"act{h}")
-            acts.append(act)
             nc.vector.tensor_copy(slot_scales[h][:], x_scale_t[:].indirect(entries(offs_t, h * HALF, HALF)))
             step = C if h == 0 else HALF
             for j0 in range(h * HALF, (h + 1) * HALF, step):
@@ -182,18 +168,21 @@ def tile_moe_two_lin_gelu_kernel(tc, xT, w_words, w_scales, b, gate, offs, dst, 
                     )
             for i in range(2):
                 e = 2 * h + i
-                n = C - TAIL if e == E - 1 else C
-                nc.scalar.activation(act[:, i * C : i * C + n], sums[i][:, :n], GELU, bias=b_t[:, e : e + 1])
-        tail = keep.tile([P, TAIL], F32, name="tail")
-        nc.scalar.activation(tail[:], sums[1][:, C - TAIL :], GELU, bias=b_t[:, E - 1 : E])
+                bias = b_t[:, e : e + 1]
+                direct = C - TAIL if e == E - 1 else C
+                nc.scalar.activation(acts[h][:, i * C : i * C + direct], sums[i][:, :direct], GELU, bias=bias)
+                if direct < C:
+                    nc.scalar.activation(act_tail[:], sums[i][:, direct:], GELU, bias=bias)
 
-        for h in range(HALVES):
-            if h == 1:
-                nc.vector.tensor_copy(acts[1][:, HALF - TAIL :], tail[:])
+        def scatter(h):
             nc.vector.tensor_tensor(
                 out_t[:].indirect(entries(dst_t, h * HALF, HALF)),
                 acts[h][:],
                 gate_t[:, h * HALF : (h + 1) * HALF],
                 MULT,
             )
+
+        scatter(0)
+        nc.vector.tensor_copy(acts[1][:, HALF - TAIL :], act_tail[:])
+        scatter(1)
         nc.sync.dma_start(out, out_t[:])

@@ -28,8 +28,7 @@ SCALE_ROWS = 4
 
 PIECES = ((0, 256), (256, 512), (512, 640))
 PASS0_VECTOR = (256, 64, 0)
-PASS1_VECTOR = (0, 128, 48)
-BRIDGE = 8
+PASS1_VECTOR = (0, 112, 64)
 TAIL = 8
 
 
@@ -124,25 +123,25 @@ def tile_moe_two_lin_gelu_kernel(tc, xT, w_words, w_scales, b, gate, offs, dst, 
             h, c0 = divmod(j0, HALF)
             nc.vector.tensor_copy(slot_words[a][h][:, c0 : c0 + n], token_words[a][:].indirect(entries(offs_t, j0, n)))
 
+        def shares(piece, vector_tokens):
+            t0, t1 = PIECES[piece]
+            border = t0 + vector_tokens[piece]
+            return [part for part in ((True, t0, border), (False, border, t1)) if part[1] < part[2]]
+
         for pair in range(ROWS // PAIR):
-            for (t0, t1), share in zip(PIECES, PASS0_VECTOR):
-                if share > 0:
-                    cast_pair(True, pair, t0, t0 + share)
-                if t0 + share < t1:
-                    cast_pair(False, pair, t0 + share, t1)
+            for piece in range(len(PIECES)):
+                for on_vector, t0, t1 in shares(piece, PASS0_VECTOR):
+                    cast_pair(on_vector, pair, t0, t1)
         for piece in range(len(PIECES)):
             quantize(0, piece)
-        first_border, second_border = PIECES[1]
-        cast_pass1(False, 0, first_border - BRIDGE)
+        for part in shares(0, PASS1_VECTOR):
+            cast_pass1(*part)
         for h in range(HALVES):
             gather_words(0, h * HALF, HALF)
-
-        cast_pass1(True, second_border - PASS1_VECTOR[1], second_border)
-        cast_pass1(False, first_border - BRIDGE, first_border + BRIDGE)
-        cast_pass1(False, first_border + BRIDGE, second_border - PASS1_VECTOR[1])
         quantize(1, 0)
-        cast_pass1(True, second_border, second_border + PASS1_VECTOR[2])
-        cast_pass1(False, second_border + PASS1_VECTOR[2], T)
+        for piece in (1, 2):
+            for part in shares(piece, PASS1_VECTOR):
+                cast_pass1(*part)
         quantize(1, 1)
         quantize(1, 2)
 

@@ -26,9 +26,7 @@ HALF = S // HALVES
 PER_COLUMN = 16
 SCALE_ROWS = 4
 
-PIECES = ((0, 256), (256, 512), (512, 640))
-PASS0_VECTOR = (256, 64, 0)
-PASS1_VECTOR = (0, 112, 64)
+SCALAR_TOKENS = (212, 352, 352, 272)
 TAIL = 8
 
 
@@ -42,21 +40,17 @@ def tile_moe_two_lin_gelu_kernel(tc, xT, w_words, w_scales, b, gate, offs, dst, 
         dst_t = keep.tile([P, S // PER_COLUMN], U16, name="dst_t")
         b_t = keep.tile([P, E], F32, name="b_t")
 
-        x_rows = xT.rearrange("(a p r) t -> a p r t", a=PASSES, r=ROWS)
-        raw_pairs = []
-        for r0 in range(0, ROWS, PAIR):
-            raw_pair = keep.tile([P, PAIR, T], F32, name=f"raw_pair{r0}")
-            nc.sync.dma_start(raw_pair[:], x_rows[0, :, r0 : r0 + PAIR, :])
-            raw_pairs.append(raw_pair)
-        nc.sync.dma_start(offs_t[:], offs)
-        raw_pass1 = keep.tile([P, ROWS, T], F32, name="raw_pass1")
-        for t0, t1 in PIECES:
-            nc.sync.dma_start(raw_pass1[:, :, t0:t1], x_rows[1, :, :, t0:t1])
+        x_rows = xT.rearrange("(a p q r) t -> a q p r t", a=PASSES, q=ROWS // PAIR, r=PAIR)
+        raw = []
+        for i in range(PASSES * ROWS // PAIR):
+            raw_pair = keep.tile([P, PAIR, T], F32, name=f"raw_pair{i}", align_bytes=64)
+            nc.sync.dma_start(raw_pair[:], x_rows[i // 2, i % 2])
+            raw.append(raw_pair)
+            if i == 0:
+                nc.sync.dma_start(offs_t[:], offs)
 
         w_scale_t = keep.tile([P, PASSES * E, N], U8, name="w_scale_t", align_bytes=64)
         nc.vector.memset(w_scale_t[:].rearrange("p g n -> p (g n)").bitcast(I32), 0)
-        x_scale_t = keep.tile([P, T], U8, name="x_scale_t", align_bytes=64)
-        nc.vector.memset(x_scale_t[:].bitcast(I32), 0)
         out_t = keep.tile([P, T], F32, name="out_t")
         nc.vector.memset(out_t[:], 0.0)
         warm = keep.tile([P, 1], F32, name="warm")
@@ -83,75 +77,80 @@ def tile_moe_two_lin_gelu_kernel(tc, xT, w_words, w_scales, b, gate, offs, dst, 
         nc.sync.dma_start(dst_t[:], dst)
         w_words_t.append(load_w_words(1))
 
-        token_words = [keep.tile([P, T], U32, name=f"token_words{a}", align_bytes=64) for a in range(PASSES)]
-        slot_words = [
-            [keep.tile([P, HALF], U32, name=f"slot_words{a}{h}", align_bytes=64) for h in range(HALVES)]
+        token_pairs = [keep.tile([P, T], U32, name=f"token_pairs{i}", align_bytes=64) for i in range(4)]
+        slot_pairs = [
+            [keep.tile([P, 2, HALF], U32, name=f"slot_pairs{a}{h}", align_bytes=64) for h in range(HALVES)]
             for a in range(PASSES)
         ]
-        slot_scales = [keep.tile([P, HALF], U8, name=f"slot_scales{h}", align_bytes=64) for h in range(HALVES)]
-        rounded = [keep.tile([P, T, ROWS], BF16, name=f"rounded{a}", align_bytes=64) for a in range(PASSES)]
+        woven = {(1, h): keep.tile([P, 2 * HALF], U32, name=f"woven1{h}", align_bytes=64) for h in range(HALVES)}
+        codes = {
+            (a, h): keep.tile([P, HALF], U32, name=f"codes{a}{h}", align_bytes=64) for a, h in ((0, 0), (1, 0), (1, 1))
+        }
+        scales = [
+            [keep.tile([P, HALF], U8, name=f"scales{a}{h}", align_bytes=64) for h in range(HALVES)]
+            for a in range(PASSES)
+        ]
 
-        def cast(on_vector, target, source):
-            if on_vector:
-                nc.vector.tensor_copy(target, source)
-            else:
-                nc.scalar.activation(target, source, COPY)
-
-        def cast_pair(on_vector, pair, t0, t1):
-            rows = slice(PAIR * pair, PAIR * (pair + 1))
-            cast(on_vector, rounded[0][:, t0:t1, rows], raw_pairs[pair][:, :, t0:t1].rearrange("p r t -> p t r"))
-
-        def cast_pass1(on_vector, t0, t1):
-            cast(
-                on_vector,
-                rounded[1][:, t0:t1, :].rearrange("p (c u) r -> p c r u", u=4),
-                raw_pass1[:, :, t0:t1].rearrange("p r (c u) -> p c r u", u=4),
-            )
-
-        def quantize(a, piece):
-            t0, t1 = PIECES[piece]
-            nc.vector.quantize_mx(
-                out=token_words[a][:, t0:t1].bitcast(FP8X4),
-                scales=x_scale_t[SCALE_ROWS * a : P, t0:t1],
-                in_=rounded[a][:, t0:t1, :].rearrange("p t r -> p (t r)"),
-            )
+        def cast(i):
+            border = T - SCALAR_TOKENS[i]
+            target = token_pairs[i][:].bitcast(BF16).rearrange("p (t r) -> p t r", r=PAIR)
+            source = raw[i][:].rearrange("p r t -> p t r")
+            other = nc.vector if i == 0 else nc.gpsimd
+            other.tensor_copy(target[:, :border, :], source[:, :border, :])
+            nc.scalar.activation(target[:, border:, :], source[:, border:, :], COPY)
 
         def entries(list_t, j0, n):
             return list_t[:, j0 // PER_COLUMN : (j0 + n) // PER_COLUMN]
 
-        def gather_words(a, j0, n):
+        def gather(i, j0, n):
             h, c0 = divmod(j0, HALF)
-            nc.vector.tensor_copy(slot_words[a][h][:, c0 : c0 + n], token_words[a][:].indirect(entries(offs_t, j0, n)))
+            nc.vector.tensor_copy(
+                slot_pairs[i // 2][h][:, i % 2, c0 : c0 + n], token_pairs[i][:].indirect(entries(offs_t, j0, n))
+            )
 
-        def shares(piece, vector_tokens):
-            t0, t1 = PIECES[piece]
-            border = t0 + vector_tokens[piece]
-            return [part for part in ((True, t0, border), (False, border, t1)) if part[1] < part[2]]
+        def weave(on_gpsimd, a, j0, n):
+            h, c0 = divmod(j0, HALF)
+            target = woven[a, h][:, 2 * c0 : 2 * (c0 + n)]
+            source = slot_pairs[a][h][:, :, c0 : c0 + n]
+            if on_gpsimd:
+                nc.gpsimd.tensor_copy(target.rearrange("p (s q) -> p s q", q=2), source.rearrange("p q s -> p s q"))
+            else:
+                nc.scalar.copy(target.rearrange("p (s q) -> p s q", q=2), source.rearrange("p q s -> p s q"))
 
-        for pair in range(ROWS // PAIR):
-            for piece in range(len(PIECES)):
-                for on_vector, t0, t1 in shares(piece, PASS0_VECTOR):
-                    cast_pair(on_vector, pair, t0, t1)
-        for piece in range(len(PIECES)):
-            quantize(0, piece)
-        for part in shares(0, PASS1_VECTOR):
-            cast_pass1(*part)
+        def quantize(a, j0, n):
+            h, c0 = divmod(j0, HALF)
+            nc.vector.quantize_mx(
+                out=codes[a, h][:, c0 : c0 + n].bitcast(FP8X4),
+                scales=scales[a][h][:, c0 : c0 + n],
+                in_=woven[a, h][:, 2 * c0 : 2 * (c0 + n)].bitcast(BF16),
+            )
+
+        for i in range(2):
+            cast(i)
+            for h in range(HALVES):
+                gather(i, h * HALF, HALF)
+        cast(2)
+        woven[0, 0] = keep.tile([P, 2 * HALF], U32, name="raw_pair2", align_bytes=64)
+        weave(False, 0, 0, HALF)
         for h in range(HALVES):
-            gather_words(0, h * HALF, HALF)
-        quantize(1, 0)
-        for piece in (1, 2):
-            for part in shares(piece, PASS1_VECTOR):
-                cast_pass1(*part)
-        quantize(1, 1)
-        quantize(1, 2)
+            gather(2, h * HALF, HALF)
+        quantize(0, 0, HALF)
+        cast(3)
+        woven[0, 1] = keep.tile([P, 2 * HALF], U32, name="raw_pair3", align_bytes=64)
+        weave(True, 0, HALF, HALF)
+        for e in range(E):
+            gather(3, e * C, C)
+            weave(False, 1, e * C, C)
+        quantize(1, 0, C)
+        quantize(1, C, C)
+        codes[0, 1] = keep.tile([P, HALF], U32, name="slot_pairs10", align_bytes=64)
+        quantize(0, HALF, HALF)
+        quantize(1, 2 * C, C)
+        quantize(1, 3 * C, C)
 
         acts = [keep.tile([P, HALF], F32, name=f"act{h}") for h in range(HALVES)]
         act_tail = keep.tile([P, TAIL], F32, name="act_tail")
         for h in range(HALVES):
-            nc.vector.tensor_copy(slot_scales[h][:], x_scale_t[:].indirect(entries(offs_t, h * HALF, HALF)))
-            step = C if h == 0 else HALF
-            for j0 in range(h * HALF, (h + 1) * HALF, step):
-                gather_words(1, j0, step)
             sums = [psum.tile([P, C], F32, name=f"sums{2 * h + i}") for i in range(2)]
             for a in range(PASSES):
                 for i in range(2):
@@ -160,8 +159,8 @@ def tile_moe_two_lin_gelu_kernel(tc, xT, w_words, w_scales, b, gate, offs, dst, 
                         out=sums[i][:],
                         lhsT=w_words_t[h][:, PASSES * i + a, :].bitcast(FP8X4),
                         lhsT_scale=w_scale_t[:, PASSES * (2 * h + i) + a, :],
-                        rhs=slot_words[a][h][:, cols].bitcast(FP8X4),
-                        rhs_scale=slot_scales[h][SCALE_ROWS * a : P, cols],
+                        rhs=codes[a, h][:, cols].bitcast(FP8X4),
+                        rhs_scale=scales[a][h][:, cols],
                         start=(a == 0),
                         stop=(a == PASSES - 1),
                     )

@@ -26,8 +26,11 @@ HALF = S // HALVES
 PER_COLUMN = 16
 SCALE_ROWS = 4
 
-SCALAR_TOKENS = (212, 352, 352, 272)
-TAIL = 8
+SCALAR_TOKENS = (212, 352)
+SPLIT = 320
+SCALAR_PARTS = ((192, 176), (144, 176))
+WINDOW = 768
+REST = S - C
 
 
 def tile_moe_two_lin_gelu_kernel(tc, xT, w_words, w_scales, b, gate, offs, dst, out):
@@ -44,143 +47,134 @@ def tile_moe_two_lin_gelu_kernel(tc, xT, w_words, w_scales, b, gate, offs, dst, 
         raw = []
         for i in range(PASSES * ROWS // PAIR):
             raw_pair = keep.tile([P, PAIR, T], F32, name=f"raw_pair{i}", align_bytes=64)
-            nc.sync.dma_start(raw_pair[:], x_rows[i // 2, i % 2])
+            if i < 2:
+                nc.sync.dma_start(raw_pair[:], x_rows[i // 2, i % 2])
+            else:
+                run = raw_pair[:].rearrange("p r t -> p (r t)")
+                source = x_rows[i // 2, i % 2].rearrange("p r t -> p (r t)")
+                nc.sync.dma_start(run[:, : T + SPLIT], source[:, : T + SPLIT])
+                nc.sync.dma_start(run[:, T + SPLIT :], source[:, T + SPLIT :])
             raw.append(raw_pair)
             if i == 0:
                 nc.sync.dma_start(offs_t[:], offs)
 
         w_scale_t = keep.tile([P, PASSES * E, N], U8, name="w_scale_t", align_bytes=64)
         nc.vector.memset(w_scale_t[:].rearrange("p g n -> p (g n)").bitcast(I32), 0)
-        out_t = keep.tile([P, T], F32, name="out_t")
+        out_t = keep.tile([P, WINDOW], F32, name="out_t")
         nc.vector.memset(out_t[:], 0.0)
         warm = keep.tile([P, 1], F32, name="warm")
         nc.vector.memset(warm[:], 0.0)
         nc.scalar.activation(warm[:], warm[:], GELU)
 
-        def load_w_words(h):
-            words = keep.tile([P, PASSES * E // HALVES, N], I32, name=f"w_words{h}", align_bytes=64)
-            nc.sync.dma_start(
-                words[:],
-                w_words[2 * h : 2 * h + 2].rearrange("e a p n r -> p (e a) (n r)").bitcast(I32),
-            )
-            return words
-
-        w_words_t = [load_w_words(0)]
+        w_words_t = keep.tile([P, PASSES * E, N], I32, name="w_words_t", align_bytes=64)
+        nc.sync.dma_start(w_words_t[:], w_words.rearrange("e a p n r -> p (e a) (n r)").bitcast(I32))
         for s0 in range(SCALE_ROWS):
             nc.sync.dma_start(
                 w_scale_t[s0:P:32, :, :].bitcast(I32),
                 w_scales[:, :, s0:16:SCALE_ROWS, :].rearrange("e a s n -> s (e a) n").bitcast(I32),
             )
-        nc.sync.dma_start(b_t[:], b)
         gate_t = keep.tile([P, S], F32, name="gate_t")
         nc.sync.dma_start(gate_t[:], gate)
         nc.sync.dma_start(dst_t[:], dst)
-        w_words_t.append(load_w_words(1))
+        nc.sync.dma_start(b_t[:], b)
 
         token_pairs = [keep.tile([P, T], U32, name=f"token_pairs{i}", align_bytes=64) for i in range(4)]
+        groups = ((0, C), (C, REST))
         slot_pairs = [
-            [keep.tile([P, 2, HALF], U32, name=f"slot_pairs{a}{h}", align_bytes=64) for h in range(HALVES)]
+            [keep.tile([P, 2, n], U32, name=f"slot_pairs{a}{g}", align_bytes=64) for g, (j0, n) in enumerate(groups)]
             for a in range(PASSES)
         ]
-        woven = {(1, h): keep.tile([P, 2 * HALF], U32, name=f"woven1{h}", align_bytes=64) for h in range(HALVES)}
+        woven1 = [keep.tile([P, 2 * C], U32, name=f"woven1{e}", align_bytes=64) for e in range(E)]
         codes = {
-            (a, h): keep.tile([P, HALF], U32, name=f"codes{a}{h}", align_bytes=64) for a, h in ((0, 0), (1, 0), (1, 1))
+            (a, g): keep.tile([P, groups[g][1]], U32, name=f"codes{a}{g}", align_bytes=64)
+            for a, g in ((0, 0), (1, 0), (1, 1))
         }
         scales = [
-            [keep.tile([P, HALF], U8, name=f"scales{a}{h}", align_bytes=64) for h in range(HALVES)]
+            [keep.tile([P, n], U8, name=f"scales{a}{g}", align_bytes=64) for g, (j0, n) in enumerate(groups)]
             for a in range(PASSES)
         ]
 
-        def cast(i):
-            border = T - SCALAR_TOKENS[i]
+        def cast_range(i, t0, t1, on_scalar):
+            border = t1 - on_scalar
             target = token_pairs[i][:].bitcast(BF16).rearrange("p (t r) -> p t r", r=PAIR)
             source = raw[i][:].rearrange("p r t -> p t r")
             other = nc.vector if i == 0 else nc.gpsimd
-            other.tensor_copy(target[:, :border, :], source[:, :border, :])
-            nc.scalar.activation(target[:, border:, :], source[:, border:, :], COPY)
+            other.tensor_copy(target[:, t0:border, :], source[:, t0:border, :])
+            nc.scalar.activation(target[:, border:t1, :], source[:, border:t1, :], COPY)
+
+        def cast(i):
+            if i < 2:
+                cast_range(i, 0, T, SCALAR_TOKENS[i])
+            else:
+                cast_range(i, 0, SPLIT, SCALAR_PARTS[i - 2][0])
+                cast_range(i, SPLIT, T, SCALAR_PARTS[i - 2][1])
 
         def entries(list_t, j0, n):
             return list_t[:, j0 // PER_COLUMN : (j0 + n) // PER_COLUMN]
 
+        def place(j0, n):
+            g = min(j0 // C, 1)
+            return g, slice(j0 - groups[g][0], j0 - groups[g][0] + n)
+
         def gather(i, j0, n):
-            h, c0 = divmod(j0, HALF)
-            nc.vector.tensor_copy(
-                slot_pairs[i // 2][h][:, i % 2, c0 : c0 + n], token_pairs[i][:].indirect(entries(offs_t, j0, n))
-            )
+            g, cols = place(j0, n)
+            nc.vector.tensor_copy(slot_pairs[i // 2][g][:, i % 2, cols], token_pairs[i][:].indirect(entries(offs_t, j0, n)))
 
-        def weave(on_gpsimd, a, j0, n):
-            h, c0 = divmod(j0, HALF)
-            target = woven[a, h][:, 2 * c0 : 2 * (c0 + n)]
-            source = slot_pairs[a][h][:, :, c0 : c0 + n]
-            if on_gpsimd:
-                nc.gpsimd.tensor_copy(target.rearrange("p (s q) -> p s q", q=2), source.rearrange("p q s -> p s q"))
-            else:
-                nc.scalar.copy(target.rearrange("p (s q) -> p s q", q=2), source.rearrange("p q s -> p s q"))
+        def weave(copy, target, a, j0, n):
+            g, cols = place(j0, n)
+            copy(target.rearrange("p (s q) -> p s q", q=2), slot_pairs[a][g][:, :, cols].rearrange("p q s -> p s q"))
 
-        def quantize(a, j0, n):
-            h, c0 = divmod(j0, HALF)
+        def quantize(a, j0, n, source):
+            g, cols = place(j0, n)
             nc.vector.quantize_mx(
-                out=codes[a, h][:, c0 : c0 + n].bitcast(FP8X4),
-                scales=scales[a][h][:, c0 : c0 + n],
-                in_=woven[a, h][:, 2 * c0 : 2 * (c0 + n)].bitcast(BF16),
+                out=codes[a, g][:, cols].bitcast(FP8X4), scales=scales[a][g][:, cols], in_=source.bitcast(BF16)
             )
 
-        for i in range(2):
+        for i in range(3):
             cast(i)
-            for h in range(HALVES):
-                gather(i, h * HALF, HALF)
-        cast(2)
-        woven[0, 0] = keep.tile([P, 2 * HALF], U32, name="raw_pair2", align_bytes=64)
-        weave(False, 0, 0, HALF)
-        for h in range(HALVES):
-            gather(2, h * HALF, HALF)
-        quantize(0, 0, HALF)
+            for j0, n in groups:
+                gather(i, j0, n)
+        woven0_first = keep.tile([P, 2 * C], U32, name="raw_pair2", align_bytes=64)
+        weave(nc.scalar.copy, woven0_first[:], 0, 0, C)
+        quantize(0, 0, C, woven0_first[:])
         cast(3)
-        woven[0, 1] = keep.tile([P, 2 * HALF], U32, name="raw_pair3", align_bytes=64)
-        weave(True, 0, HALF, HALF)
+        woven0_rest = keep.tile([P, 2 * REST], U32, name="raw_pair3", align_bytes=64)
+        weave(nc.gpsimd.tensor_copy, woven0_rest[:], 0, C, REST)
         for e in range(E):
             gather(3, e * C, C)
-            weave(False, 1, e * C, C)
-        quantize(1, 0, C)
-        quantize(1, C, C)
-        codes[0, 1] = keep.tile([P, HALF], U32, name="slot_pairs10", align_bytes=64)
-        quantize(0, HALF, HALF)
-        quantize(1, 2 * C, C)
-        quantize(1, 3 * C, C)
+            weave(nc.scalar.copy, woven1[e][:], 1, e * C, C)
+        quantize(1, 0, C, woven1[0][:])
+        codes[0, 1] = keep.tile([P, REST], U32, name="slot_pairs10", align_bytes=64)
+        quantize(0, C, C, woven0_rest[:, : 2 * C])
+        quantize(0, 2 * C, 2 * C, woven0_rest[:, 2 * C :])
+        for e in range(1, E):
+            quantize(1, e * C, C, woven1[e][:])
 
-        acts = [keep.tile([P, HALF], F32, name=f"act{h}") for h in range(HALVES)]
-        act_tail = keep.tile([P, TAIL], F32, name="act_tail")
-        for h in range(HALVES):
-            sums = [psum.tile([P, C], F32, name=f"sums{2 * h + i}") for i in range(2)]
+        acts = [keep.tile([P, n], F32, name=f"act{g}") for g, (j0, n) in enumerate(groups)]
+        sums = [psum.tile([P, C], F32, name=f"sums{e}") for e in range(E)]
+        for experts in ((0,), (1, 2, 3)):
             for a in range(PASSES):
-                for i in range(2):
-                    cols = slice(i * C, (i + 1) * C)
+                for e in experts:
+                    g, cols = place(e * C, C)
                     nc.tensor.matmul_mx(
-                        out=sums[i][:],
-                        lhsT=w_words_t[h][:, PASSES * i + a, :].bitcast(FP8X4),
-                        lhsT_scale=w_scale_t[:, PASSES * (2 * h + i) + a, :],
-                        rhs=codes[a, h][:, cols].bitcast(FP8X4),
-                        rhs_scale=scales[a][h][:, cols],
+                        out=sums[e][:],
+                        lhsT=w_words_t[:, PASSES * e + a, :].bitcast(FP8X4),
+                        lhsT_scale=w_scale_t[:, PASSES * e + a, :],
+                        rhs=codes[a, g][:, cols].bitcast(FP8X4),
+                        rhs_scale=scales[a][g][:, cols],
                         start=(a == 0),
                         stop=(a == PASSES - 1),
                     )
-            for i in range(2):
-                e = 2 * h + i
-                bias = b_t[:, e : e + 1]
-                direct = C - TAIL if e == E - 1 else C
-                nc.scalar.activation(acts[h][:, i * C : i * C + direct], sums[i][:, :direct], GELU, bias=bias)
-                if direct < C:
-                    nc.scalar.activation(act_tail[:], sums[i][:, direct:], GELU, bias=bias)
+            for e in experts:
+                g, cols = place(e * C, C)
+                nc.scalar.activation(acts[g][:, cols], sums[e][:], GELU, bias=b_t[:, e : e + 1])
 
-        def scatter(h):
+        def scatter(g):
+            j0, n = groups[g]
             nc.vector.tensor_tensor(
-                out_t[:].indirect(entries(dst_t, h * HALF, HALF)),
-                acts[h][:],
-                gate_t[:, h * HALF : (h + 1) * HALF],
-                MULT,
+                out_t[:].indirect(entries(dst_t, j0, n)), acts[g][:], gate_t[:, j0 : j0 + n], MULT
             )
 
         scatter(0)
-        nc.vector.tensor_copy(acts[1][:, HALF - TAIL :], act_tail[:])
         scatter(1)
-        nc.sync.dma_start(out, out_t[:])
+        nc.sync.dma_start(out, out_t[:, :T])

@@ -66,17 +66,17 @@ def tile_moe_two_lin_gelu_kernel(tc, xT, w_words, w_scales, b, gate, offs, dst, 
         nc.vector.memset(warm[:], 0.0)
         nc.scalar.activation(warm[:], warm[:], GELU)
 
-        w_words_t = keep.tile([P, PASSES * E, N], I32, name="w_words_t", align_bytes=64)
-        nc.sync.dma_start(w_words_t[:], w_words.rearrange("e a p n r -> p (e a) (n r)").bitcast(I32))
         for s0 in range(SCALE_ROWS):
             nc.sync.dma_start(
                 w_scale_t[s0:P:32, :, :].bitcast(I32),
                 w_scales[:, :, s0:16:SCALE_ROWS, :].rearrange("e a s n -> s (e a) n").bitcast(I32),
             )
+        w_words_t = keep.tile([P, PASSES * E, N], I32, name="w_words_t", align_bytes=64)
+        nc.sync.dma_start(w_words_t[:], w_words.rearrange("e a p n r -> p (e a) (n r)").bitcast(I32))
+        nc.sync.dma_start(b_t[:], b)
+        nc.sync.dma_start(dst_t[:], dst)
         gate_t = keep.tile([P, S], F32, name="gate_t")
         nc.sync.dma_start(gate_t[:], gate)
-        nc.sync.dma_start(dst_t[:], dst)
-        nc.sync.dma_start(b_t[:], b)
 
         token_pairs = [keep.tile([P, T], U32, name=f"token_pairs{i}", align_bytes=64) for i in range(4)]
         groups = ((0, C), (C, REST))
@@ -139,14 +139,15 @@ def tile_moe_two_lin_gelu_kernel(tc, xT, w_words, w_scales, b, gate, offs, dst, 
         quantize(0, 0, C, woven0_first[:])
         cast(3)
         woven0_rest = keep.tile([P, 2 * REST], U32, name="raw_pair3", align_bytes=64)
-        weave(nc.gpsimd.tensor_copy, woven0_rest[:], 0, C, REST)
+        weave(nc.scalar.copy, woven0_rest[:, : 4 * C], 0, C, 2 * C)
+        weave(nc.gpsimd.tensor_copy, woven0_rest[:, 4 * C :], 0, 3 * C, C)
         for e in range(E):
             gather(3, e * C, C)
             weave(nc.scalar.copy, woven1[e][:], 1, e * C, C)
         quantize(1, 0, C, woven1[0][:])
         codes[0, 1] = keep.tile([P, REST], U32, name="slot_pairs10", align_bytes=64)
-        quantize(0, C, C, woven0_rest[:, : 2 * C])
-        quantize(0, 2 * C, 2 * C, woven0_rest[:, 2 * C :])
+        quantize(0, C, 2 * C, woven0_rest[:, : 4 * C])
+        quantize(0, 3 * C, C, woven0_rest[:, 4 * C :])
         for e in range(1, E):
             quantize(1, e * C, C, woven1[e][:])
 

@@ -26,9 +26,9 @@ HALF = S // HALVES
 PER_COLUMN = 16
 SCALE_ROWS = 4
 
-SCALAR_TOKENS = (212, 352)
-SPLIT = 320
-SCALAR_PARTS = ((192, 176), (144, 176))
+SCALAR_TOKENS = (212, 392)
+SPLIT = 400
+SCALAR_PARTS = ((144, 240), (112, 240))
 WINDOW = 768
 REST = S - C
 
@@ -99,7 +99,8 @@ def tile_moe_two_lin_gelu_kernel(tc, xT, w_words, w_scales, b, gate, offs, dst, 
             target = token_pairs[i][:].bitcast(BF16).rearrange("p (t r) -> p t r", r=PAIR)
             source = raw[i][:].rearrange("p r t -> p t r")
             other = nc.vector if i == 0 else nc.gpsimd
-            other.tensor_copy(target[:, t0:border, :], source[:, t0:border, :])
+            if border > t0:
+                other.tensor_copy(target[:, t0:border, :], source[:, t0:border, :])
             nc.scalar.activation(target[:, border:t1, :], source[:, border:t1, :], COPY)
 
         def cast(i):
@@ -139,8 +140,7 @@ def tile_moe_two_lin_gelu_kernel(tc, xT, w_words, w_scales, b, gate, offs, dst, 
         quantize(0, 0, C, woven0_first[:])
         cast(3)
         woven0_rest = keep.tile([P, 2 * REST], U32, name="raw_pair3", align_bytes=64)
-        weave(nc.scalar.copy, woven0_rest[:, : 4 * C], 0, C, 2 * C)
-        weave(nc.gpsimd.tensor_copy, woven0_rest[:, 4 * C :], 0, 3 * C, C)
+        weave(nc.scalar.copy, woven0_rest[:], 0, C, REST)
         for e in range(E):
             gather(3, e * C, C)
             weave(nc.scalar.copy, woven1[e][:], 1, e * C, C)

@@ -66,13 +66,13 @@ def tile_moe_two_lin_gelu_kernel(tc, xT, w_words, w_scales, b, gate, offs, dst, 
         nc.vector.memset(warm[:], 0.0)
         nc.scalar.activation(warm[:], warm[:], GELU)
 
+        w_words_t = keep.tile([P, PASSES * E, N], I32, name="w_words_t", align_bytes=64)
+        nc.sync.dma_start(w_words_t[:], w_words.rearrange("e a p n r -> p (e a) (n r)").bitcast(I32))
         for s0 in range(SCALE_ROWS):
             nc.sync.dma_start(
                 w_scale_t[s0:P:32, :, :].bitcast(I32),
                 w_scales[:, :, s0:16:SCALE_ROWS, :].rearrange("e a s n -> s (e a) n").bitcast(I32),
             )
-        w_words_t = keep.tile([P, PASSES * E, N], I32, name="w_words_t", align_bytes=64)
-        nc.sync.dma_start(w_words_t[:], w_words.rearrange("e a p n r -> p (e a) (n r)").bitcast(I32))
         nc.sync.dma_start(b_t[:], b)
         nc.sync.dma_start(dst_t[:], dst)
         gate_t = keep.tile([P, S], F32, name="gate_t")

@@ -26,9 +26,9 @@ HALF = S // HALVES
 PER_COLUMN = 16
 SCALE_ROWS = 4
 
-SCALAR_TOKENS = (212, 392)
-SPLIT = 400
-SCALAR_PARTS = ((144, 240), (112, 240))
+SCALAR_TOKENS = (212, 440)
+SPLIT = 352
+SCALAR_PARTS = ((128, 288), (128, 288))
 WINDOW = 768
 REST = S - C
 
@@ -131,13 +131,16 @@ def tile_moe_two_lin_gelu_kernel(tc, xT, w_words, w_scales, b, gate, offs, dst, 
                 out=codes[a, g][:, cols].bitcast(FP8X4), scales=scales[a][g][:, cols], in_=source.bitcast(BF16)
             )
 
+        woven0_first = keep.tile([P, C, 2], U32, name="woven0_first", align_bytes=64)
         for i in range(3):
             cast(i)
-            for j0, n in groups:
-                gather(i, j0, n)
-        woven0_first = keep.tile([P, 2 * C], U32, name="raw_pair2", align_bytes=64)
-        weave(nc.scalar.copy, woven0_first[:], 0, 0, C)
-        quantize(0, 0, C, woven0_first[:])
+            if i < 2:
+                nc.vector.tensor_copy(woven0_first[:, :, i], token_pairs[i][:].indirect(entries(offs_t, 0, C)))
+            else:
+                gather(i, 0, C)
+            gather(i, C, REST)
+            if i == 1:
+                quantize(0, 0, C, woven0_first[:].rearrange("p s q -> p (s q)"))
         cast(3)
         woven0_rest = keep.tile([P, 2 * REST], U32, name="raw_pair3", align_bytes=64)
         weave(nc.scalar.copy, woven0_rest[:], 0, C, REST)

@@ -26,9 +26,9 @@ HALF = S // HALVES
 PER_COLUMN = 16
 SCALE_ROWS = 4
 
-SCALAR_TOKENS = (212, 440)
-SPLIT = 352
-SCALAR_PARTS = ((128, 288), (128, 288))
+SCALAR_TOKENS = (212, 376)
+SPLITS = (400, 432)
+SCALAR_PARTS = ((144, 240), (128, 208))
 WINDOW = 768
 REST = S - C
 
@@ -52,8 +52,9 @@ def tile_moe_two_lin_gelu_kernel(tc, xT, w_words, w_scales, b, gate, offs, dst, 
             else:
                 run = raw_pair[:].rearrange("p r t -> p (r t)")
                 source = x_rows[i // 2, i % 2].rearrange("p r t -> p (r t)")
-                nc.sync.dma_start(run[:, : T + SPLIT], source[:, : T + SPLIT])
-                nc.sync.dma_start(run[:, T + SPLIT :], source[:, T + SPLIT :])
+                border = T + SPLITS[i - 2]
+                nc.sync.dma_start(run[:, :border], source[:, :border])
+                nc.sync.dma_start(run[:, border:], source[:, border:])
             raw.append(raw_pair)
             if i == 0:
                 nc.sync.dma_start(offs_t[:], offs)
@@ -87,7 +88,7 @@ def tile_moe_two_lin_gelu_kernel(tc, xT, w_words, w_scales, b, gate, offs, dst, 
         woven1 = [keep.tile([P, 2 * C], U32, name=f"woven1{e}", align_bytes=64) for e in range(E)]
         codes = {
             (a, g): keep.tile([P, groups[g][1]], U32, name=f"codes{a}{g}", align_bytes=64)
-            for a, g in ((0, 0), (1, 0), (1, 1))
+            for a, g in ((1, 0), (1, 1))
         }
         scales = [
             [keep.tile([P, n], U8, name=f"scales{a}{g}", align_bytes=64) for g, (j0, n) in enumerate(groups)]
@@ -107,8 +108,8 @@ def tile_moe_two_lin_gelu_kernel(tc, xT, w_words, w_scales, b, gate, offs, dst, 
             if i < 2:
                 cast_range(i, 0, T, SCALAR_TOKENS[i])
             else:
-                cast_range(i, 0, SPLIT, SCALAR_PARTS[i - 2][0])
-                cast_range(i, SPLIT, T, SCALAR_PARTS[i - 2][1])
+                cast_range(i, 0, SPLITS[i - 2], SCALAR_PARTS[i - 2][0])
+                cast_range(i, SPLITS[i - 2], T, SCALAR_PARTS[i - 2][1])
 
         def entries(list_t, j0, n):
             return list_t[:, j0 // PER_COLUMN : (j0 + n) // PER_COLUMN]
@@ -134,12 +135,17 @@ def tile_moe_two_lin_gelu_kernel(tc, xT, w_words, w_scales, b, gate, offs, dst, 
         woven0_first = keep.tile([P, C, 2], U32, name="woven0_first", align_bytes=64)
         for i in range(3):
             cast(i)
-            if i < 2:
+            if i == 0:
                 nc.vector.tensor_copy(woven0_first[:, :, i], token_pairs[i][:].indirect(entries(offs_t, 0, C)))
+            elif i == 1:
+                values = woven0_first[:].rearrange("p s q -> p (s q)").bitcast(BF16).rearrange("p (s r) -> p s r", r=ROWS)
+                for r in range(PAIR):
+                    nc.vector.tensor_copy(values[:, :, PAIR + r], raw[i][:, r, :].indirect(entries(offs_t, 0, C)))
             else:
                 gather(i, 0, C)
             gather(i, C, REST)
             if i == 1:
+                codes[0, 0] = keep.tile([P, C], U32, name="raw_pair1", align_bytes=64)
                 quantize(0, 0, C, woven0_first[:].rearrange("p s q -> p (s q)"))
         cast(3)
         woven0_rest = keep.tile([P, 2 * REST], U32, name="raw_pair3", align_bytes=64)

@@ -26,9 +26,9 @@ HALF = S // HALVES
 PER_COLUMN = 16
 SCALE_ROWS = 4
 
-SCALAR_TOKENS = (212, 376)
-SPLITS = (400, 432)
-SCALAR_PARTS = ((144, 240), (128, 208))
+SCALAR_TOKENS = (360, 360)
+SPLITS = (432, 432)
+SCALAR_PARTS = ((128, 208), (128, 208))
 WINDOW = 768
 REST = S - C
 
@@ -99,7 +99,7 @@ def tile_moe_two_lin_gelu_kernel(tc, xT, w_words, w_scales, b, gate, offs, dst, 
             border = t1 - on_scalar
             target = token_pairs[i][:].bitcast(BF16).rearrange("p (t r) -> p t r", r=PAIR)
             source = raw[i][:].rearrange("p r t -> p t r")
-            other = nc.vector if i == 0 else nc.gpsimd
+            other = nc.gpsimd
             if border > t0:
                 other.tensor_copy(target[:, t0:border, :], source[:, t0:border, :])
             nc.scalar.activation(target[:, border:t1, :], source[:, border:t1, :], COPY)
@@ -135,12 +135,10 @@ def tile_moe_two_lin_gelu_kernel(tc, xT, w_words, w_scales, b, gate, offs, dst, 
         woven0_first = keep.tile([P, C, 2], U32, name="woven0_first", align_bytes=64)
         for i in range(3):
             cast(i)
-            if i == 0:
-                nc.vector.tensor_copy(woven0_first[:, :, i], token_pairs[i][:].indirect(entries(offs_t, 0, C)))
-            elif i == 1:
+            if i < 2:
                 values = woven0_first[:].rearrange("p s q -> p (s q)").bitcast(BF16).rearrange("p (s r) -> p s r", r=ROWS)
                 for r in range(PAIR):
-                    nc.vector.tensor_copy(values[:, :, PAIR + r], raw[i][:, r, :].indirect(entries(offs_t, 0, C)))
+                    nc.vector.tensor_copy(values[:, :, PAIR * i + r], raw[i][:, r, :].indirect(entries(offs_t, 0, C)))
             else:
                 gather(i, 0, C)
             gather(i, C, REST)

@@ -26,9 +26,9 @@ HALF = S // HALVES
 PER_COLUMN = 16
 SCALE_ROWS = 4
 
-SCALAR_TOKENS = (360, 360)
-SPLITS = (432, 432)
-SCALAR_PARTS = ((128, 208), (128, 208))
+SCALAR_TOKENS = (360, 360, 360)
+SPLIT = 432
+SCALAR_PARTS = (128, 208)
 WINDOW = 768
 REST = S - C
 
@@ -47,12 +47,12 @@ def tile_moe_two_lin_gelu_kernel(tc, xT, w_words, w_scales, b, gate, offs, dst, 
         raw = []
         for i in range(PASSES * ROWS // PAIR):
             raw_pair = keep.tile([P, PAIR, T], F32, name=f"raw_pair{i}", align_bytes=64)
-            if i < 2:
+            if i < 3:
                 nc.sync.dma_start(raw_pair[:], x_rows[i // 2, i % 2])
             else:
                 run = raw_pair[:].rearrange("p r t -> p (r t)")
                 source = x_rows[i // 2, i % 2].rearrange("p r t -> p (r t)")
-                border = T + SPLITS[i - 2]
+                border = T + SPLIT
                 nc.sync.dma_start(run[:, :border], source[:, :border])
                 nc.sync.dma_start(run[:, border:], source[:, border:])
             raw.append(raw_pair)
@@ -67,17 +67,23 @@ def tile_moe_two_lin_gelu_kernel(tc, xT, w_words, w_scales, b, gate, offs, dst, 
         nc.vector.memset(warm[:], 0.0)
         nc.scalar.activation(warm[:], warm[:], GELU)
 
-        w_words_t = keep.tile([P, PASSES * E, N], I32, name="w_words_t", align_bytes=64)
-        nc.sync.dma_start(w_words_t[:], w_words.rearrange("e a p n r -> p (e a) (n r)").bitcast(I32))
+        w_rows = w_words.rearrange("e a p n r -> p (e a) (n r)").bitcast(I32)
+        w_first = keep.tile([P, PASSES * 2, N], I32, name="w_first", align_bytes=64)
+        w_rest = keep.tile([P, PASSES * (E - 2), N], I32, name="w_rest", align_bytes=64)
+        nc.sync.dma_start(w_first[:], w_rows[:, : PASSES * 2, :])
         for s0 in range(SCALE_ROWS):
             nc.sync.dma_start(
                 w_scale_t[s0:P:32, :, :].bitcast(I32),
                 w_scales[:, :, s0:16:SCALE_ROWS, :].rearrange("e a s n -> s (e a) n").bitcast(I32),
             )
+        nc.sync.dma_start(w_rest[:], w_rows[:, PASSES * 2 :, :])
         nc.sync.dma_start(b_t[:], b)
-        nc.sync.dma_start(dst_t[:], dst)
         gate_t = keep.tile([P, S], F32, name="gate_t")
         nc.sync.dma_start(gate_t[:], gate)
+        nc.sync.dma_start(dst_t[:], dst)
+
+        def weights(a, e):
+            return w_first[:, PASSES * e + a, :] if e < 2 else w_rest[:, PASSES * (e - 2) + a, :]
 
         token_pairs = [keep.tile([P, T], U32, name=f"token_pairs{i}", align_bytes=64) for i in range(4)]
         groups = ((0, C), (C, REST))
@@ -105,11 +111,11 @@ def tile_moe_two_lin_gelu_kernel(tc, xT, w_words, w_scales, b, gate, offs, dst, 
             nc.scalar.activation(target[:, border:t1, :], source[:, border:t1, :], COPY)
 
         def cast(i):
-            if i < 2:
+            if i < 3:
                 cast_range(i, 0, T, SCALAR_TOKENS[i])
             else:
-                cast_range(i, 0, SPLITS[i - 2], SCALAR_PARTS[i - 2][0])
-                cast_range(i, SPLITS[i - 2], T, SCALAR_PARTS[i - 2][1])
+                cast_range(i, 0, SPLIT, SCALAR_PARTS[0])
+                cast_range(i, SPLIT, T, SCALAR_PARTS[1])
 
         def entries(list_t, j0, n):
             return list_t[:, j0 // PER_COLUMN : (j0 + n) // PER_COLUMN]
@@ -166,7 +172,7 @@ def tile_moe_two_lin_gelu_kernel(tc, xT, w_words, w_scales, b, gate, offs, dst, 
                     g, cols = place(e * C, C)
                     nc.tensor.matmul_mx(
                         out=sums[e][:],
-                        lhsT=w_words_t[:, PASSES * e + a, :].bitcast(FP8X4),
+                        lhsT=weights(a, e).bitcast(FP8X4),
                         lhsT_scale=w_scale_t[:, PASSES * e + a, :],
                         rhs=codes[a, g][:, cols].bitcast(FP8X4),
                         rhs_scale=scales[a][g][:, cols],

@@ -21,16 +21,19 @@ MULT = mybir.AluOpType.mult
 PASSES = 2
 ROWS = 4
 PAIR = 2
-HALVES = 2
-HALF = S // HALVES
+PAIRS = PASSES * ROWS // PAIR
+LAST = PAIRS - 1
 PER_COLUMN = 16
+QUADRANT = 32
 SCALE_ROWS = 4
-
-SCALAR_TOKENS = (360, 360, 360)
-SPLIT = 432
-SCALAR_PARTS = (128, 208)
-WINDOW = 768
+EARLY = 2
 REST = S - C
+GROUPS = ((0, C), (C, REST))
+WINDOW = 2 * REST
+
+GPSIMD_TOKENS = 304
+SPLIT = 432
+GPSIMD_TOKENS_LAST = 328
 
 
 def tile_moe_two_lin_gelu_kernel(tc, xT, w_words, w_scales, b, gate, offs, dst, out):
@@ -43,18 +46,17 @@ def tile_moe_two_lin_gelu_kernel(tc, xT, w_words, w_scales, b, gate, offs, dst, 
         dst_t = keep.tile([P, S // PER_COLUMN], U16, name="dst_t")
         b_t = keep.tile([P, E], F32, name="b_t")
 
-        x_rows = xT.rearrange("(a p q r) t -> a q p r t", a=PASSES, q=ROWS // PAIR, r=PAIR)
+        x_rows = xT.rearrange("(a p q r) t -> a q p r t", a=PASSES, q=PAIR, r=PAIR)
         raw = []
-        for i in range(PASSES * ROWS // PAIR):
+        for i in range(PAIRS):
             raw_pair = keep.tile([P, PAIR, T], F32, name=f"raw_pair{i}", align_bytes=64)
-            if i < 3:
-                nc.sync.dma_start(raw_pair[:], x_rows[i // 2, i % 2])
+            if i < LAST:
+                nc.sync.dma_start(raw_pair[:], x_rows[i // PAIR, i % PAIR])
             else:
                 run = raw_pair[:].rearrange("p r t -> p (r t)")
-                source = x_rows[i // 2, i % 2].rearrange("p r t -> p (r t)")
-                border = T + SPLIT
-                nc.sync.dma_start(run[:, :border], source[:, :border])
-                nc.sync.dma_start(run[:, border:], source[:, border:])
+                source = x_rows[i // PAIR, i % PAIR].rearrange("p r t -> p (r t)")
+                nc.sync.dma_start(run[:, : T + SPLIT], source[:, : T + SPLIT])
+                nc.sync.dma_start(run[:, T + SPLIT :], source[:, T + SPLIT :])
             raw.append(raw_pair)
             if i == 0:
                 nc.sync.dma_start(offs_t[:], offs)
@@ -62,111 +64,106 @@ def tile_moe_two_lin_gelu_kernel(tc, xT, w_words, w_scales, b, gate, offs, dst, 
         w_scale_t = keep.tile([P, PASSES * E, N], U8, name="w_scale_t", align_bytes=64)
         nc.vector.memset(w_scale_t[:].rearrange("p g n -> p (g n)").bitcast(I32), 0)
         out_t = keep.tile([P, WINDOW], F32, name="out_t")
-        nc.vector.memset(out_t[:], 0.0)
+        nc.vector.memset(out_t[:, :T], 0.0)
         warm = keep.tile([P, 1], F32, name="warm")
         nc.vector.memset(warm[:], 0.0)
         nc.scalar.activation(warm[:], warm[:], GELU)
 
         w_rows = w_words.rearrange("e a p n r -> p (e a) (n r)").bitcast(I32)
-        w_first = keep.tile([P, PASSES * 2, N], I32, name="w_first", align_bytes=64)
-        w_rest = keep.tile([P, PASSES * (E - 2), N], I32, name="w_rest", align_bytes=64)
-        nc.sync.dma_start(w_first[:], w_rows[:, : PASSES * 2, :])
+        w_early = keep.tile([P, PASSES * EARLY, N], I32, name="w_early", align_bytes=64)
+        w_late = keep.tile([P, PASSES * (E - EARLY), N], I32, name="w_late", align_bytes=64)
+        nc.sync.dma_start(w_early[:], w_rows[:, : PASSES * EARLY, :])
         for s0 in range(SCALE_ROWS):
             nc.sync.dma_start(
-                w_scale_t[s0:P:32, :, :].bitcast(I32),
-                w_scales[:, :, s0:16:SCALE_ROWS, :].rearrange("e a s n -> s (e a) n").bitcast(I32),
+                w_scale_t[s0:P:QUADRANT, :, :].bitcast(I32),
+                w_scales[:, :, s0::SCALE_ROWS, :].rearrange("e a s n -> s (e a) n").bitcast(I32),
             )
-        nc.sync.dma_start(w_rest[:], w_rows[:, PASSES * 2 :, :])
+        nc.sync.dma_start(w_late[:], w_rows[:, PASSES * EARLY :, :])
         nc.sync.dma_start(b_t[:], b)
         gate_t = keep.tile([P, S], F32, name="gate_t")
         nc.sync.dma_start(gate_t[:], gate)
         nc.sync.dma_start(dst_t[:], dst)
 
         def weights(a, e):
-            return w_first[:, PASSES * e + a, :] if e < 2 else w_rest[:, PASSES * (e - 2) + a, :]
+            return w_early[:, PASSES * e + a, :] if e < EARLY else w_late[:, PASSES * (e - EARLY) + a, :]
 
-        token_pairs = [keep.tile([P, T], U32, name=f"token_pairs{i}", align_bytes=64) for i in range(4)]
-        groups = ((0, C), (C, REST))
-        slot_pairs = [
-            [keep.tile([P, 2, n], U32, name=f"slot_pairs{a}{g}", align_bytes=64) for g, (j0, n) in enumerate(groups)]
-            for a in range(PASSES)
-        ]
-        woven1 = [keep.tile([P, 2 * C], U32, name=f"woven1{e}", align_bytes=64) for e in range(E)]
+        token_pairs = [keep.tile([P, T], U32, name=f"token_pairs{i}", align_bytes=64) for i in range(PAIRS)]
+        slot_pairs = {
+            (a, g): keep.tile([P, PAIR, GROUPS[g][1]], U32, name=f"slot_pairs{a}{g}", align_bytes=64)
+            for a, g in ((0, 1), (1, 0), (1, 1))
+        }
+        woven1 = [keep.tile([P, PAIR * C], U32, name=f"woven1{e}", align_bytes=64) for e in range(E)]
         codes = {
-            (a, g): keep.tile([P, groups[g][1]], U32, name=f"codes{a}{g}", align_bytes=64)
-            for a, g in ((1, 0), (1, 1))
+            (1, g): keep.tile([P, n], U32, name=f"codes1{g}", align_bytes=64) for g, (j0, n) in enumerate(GROUPS)
         }
         scales = [
-            [keep.tile([P, n], U8, name=f"scales{a}{g}", align_bytes=64) for g, (j0, n) in enumerate(groups)]
+            [keep.tile([P, n], U8, name=f"scales{a}{g}", align_bytes=64) for g, (j0, n) in enumerate(GROUPS)]
             for a in range(PASSES)
         ]
 
-        def cast_range(i, t0, t1, on_scalar):
-            border = t1 - on_scalar
+        def round_pair(i):
             target = token_pairs[i][:].bitcast(BF16).rearrange("p (t r) -> p t r", r=PAIR)
             source = raw[i][:].rearrange("p r t -> p t r")
-            other = nc.gpsimd
-            if border > t0:
-                other.tensor_copy(target[:, t0:border, :], source[:, t0:border, :])
-            nc.scalar.activation(target[:, border:t1, :], source[:, border:t1, :], COPY)
-
-        def cast(i):
-            if i < 3:
-                cast_range(i, 0, T, SCALAR_TOKENS[i])
-            else:
-                cast_range(i, 0, SPLIT, SCALAR_PARTS[0])
-                cast_range(i, SPLIT, T, SCALAR_PARTS[1])
+            borders = (GPSIMD_TOKENS, T) if i < LAST else (GPSIMD_TOKENS_LAST, SPLIT, T)
+            nc.gpsimd.tensor_copy(target[:, : borders[0], :], source[:, : borders[0], :])
+            for t0, t1 in zip(borders, borders[1:]):
+                nc.scalar.activation(target[:, t0:t1, :], source[:, t0:t1, :], COPY)
 
         def entries(list_t, j0, n):
             return list_t[:, j0 // PER_COLUMN : (j0 + n) // PER_COLUMN]
 
         def place(j0, n):
             g = min(j0 // C, 1)
-            return g, slice(j0 - groups[g][0], j0 - groups[g][0] + n)
+            return g, slice(j0 - GROUPS[g][0], j0 - GROUPS[g][0] + n)
 
         def gather(i, j0, n):
             g, cols = place(j0, n)
-            nc.vector.tensor_copy(slot_pairs[i // 2][g][:, i % 2, cols], token_pairs[i][:].indirect(entries(offs_t, j0, n)))
-
-        def weave(copy, target, a, j0, n):
-            g, cols = place(j0, n)
-            copy(target.rearrange("p (s q) -> p s q", q=2), slot_pairs[a][g][:, :, cols].rearrange("p q s -> p s q"))
-
-        def quantize(a, j0, n, source):
-            g, cols = place(j0, n)
-            nc.vector.quantize_mx(
-                out=codes[a, g][:, cols].bitcast(FP8X4), scales=scales[a][g][:, cols], in_=source.bitcast(BF16)
+            nc.vector.tensor_copy(
+                slot_pairs[i // PAIR, g][:, i % PAIR, cols], token_pairs[i][:].indirect(entries(offs_t, j0, n))
             )
 
-        woven0_first = keep.tile([P, C, 2], U32, name="woven0_first", align_bytes=64)
-        for i in range(3):
-            cast(i)
-            if i < 2:
-                values = woven0_first[:].rearrange("p s q -> p (s q)").bitcast(BF16).rearrange("p (s r) -> p s r", r=ROWS)
-                for r in range(PAIR):
-                    nc.vector.tensor_copy(values[:, :, PAIR * i + r], raw[i][:, r, :].indirect(entries(offs_t, 0, C)))
-            else:
-                gather(i, 0, C)
+        def weave(target, a, j0, n):
+            g, cols = place(j0, n)
+            nc.scalar.copy(
+                target.rearrange("p (s q) -> p s q", q=PAIR), slot_pairs[a, g][:, :, cols].rearrange("p q s -> p s q")
+            )
+
+        def quantize(a, j0, n, woven):
+            g, cols = place(j0, n)
+            nc.vector.quantize_mx(
+                out=codes[a, g][:, cols].bitcast(FP8X4), scales=scales[a][g][:, cols], in_=woven.bitcast(BF16)
+            )
+
+        woven0_first = keep.tile([P, PAIR * C], U32, name="woven0_first", align_bytes=64)
+        values = woven0_first[:].bitcast(BF16).rearrange("p (s r) -> p s r", r=ROWS)
+        for i in range(PAIR):
+            round_pair(i)
+            for r in range(PAIR):
+                nc.vector.tensor_copy(values[:, :, PAIR * i + r], raw[i][:, r, :].indirect(entries(offs_t, 0, C)))
             gather(i, C, REST)
-            if i == 1:
-                codes[0, 0] = keep.tile([P, C], U32, name="raw_pair1", align_bytes=64)
-                quantize(0, 0, C, woven0_first[:].rearrange("p s q -> p (s q)"))
-        cast(3)
-        woven0_rest = keep.tile([P, 2 * REST], U32, name="raw_pair3", align_bytes=64)
-        weave(nc.scalar.copy, woven0_rest[:], 0, C, REST)
+        codes[0, 0] = keep.tile([P, C], U32, name="raw_pair1", align_bytes=64)
+        quantize(0, 0, C, woven0_first[:])
+
+        round_pair(PAIR)
+        for j0, n in GROUPS:
+            gather(PAIR, j0, n)
+        round_pair(LAST)
+        woven0_rest = keep.tile([P, PAIR * REST], U32, name=f"raw_pair{LAST}", align_bytes=64)
+        weave(woven0_rest[:], 0, C, REST)
         for e in range(E):
-            gather(3, e * C, C)
-            weave(nc.scalar.copy, woven1[e][:], 1, e * C, C)
+            gather(LAST, e * C, C)
+            weave(woven1[e][:], 1, e * C, C)
         quantize(1, 0, C, woven1[0][:])
         codes[0, 1] = keep.tile([P, REST], U32, name="slot_pairs10", align_bytes=64)
-        quantize(0, C, 2 * C, woven0_rest[:, : 4 * C])
-        quantize(0, 3 * C, C, woven0_rest[:, 4 * C :])
+        quantize(0, C, 2 * C, woven0_rest[:, : PAIR * 2 * C])
+        quantize(0, 3 * C, C, woven0_rest[:, PAIR * 2 * C :])
         for e in range(1, E):
             quantize(1, e * C, C, woven1[e][:])
 
-        acts = [keep.tile([P, n], F32, name=f"act{g}") for g, (j0, n) in enumerate(groups)]
+        acts = [keep.tile([P, n], F32, name=f"act{g}") for g, (j0, n) in enumerate(GROUPS)]
         sums = [psum.tile([P, C], F32, name=f"sums{e}") for e in range(E)]
-        for experts in ((0,), (1, 2, 3)):
+        for j0, n in GROUPS:
+            experts = range(j0 // C, (j0 + n) // C)
             for a in range(PASSES):
                 for e in experts:
                     g, cols = place(e * C, C)
@@ -183,12 +180,6 @@ def tile_moe_two_lin_gelu_kernel(tc, xT, w_words, w_scales, b, gate, offs, dst, 
                 g, cols = place(e * C, C)
                 nc.scalar.activation(acts[g][:, cols], sums[e][:], GELU, bias=b_t[:, e : e + 1])
 
-        def scatter(g):
-            j0, n = groups[g]
-            nc.vector.tensor_tensor(
-                out_t[:].indirect(entries(dst_t, j0, n)), acts[g][:], gate_t[:, j0 : j0 + n], MULT
-            )
-
-        scatter(0)
-        scatter(1)
+        for g, (j0, n) in enumerate(GROUPS):
+            nc.vector.tensor_tensor(out_t[:].indirect(entries(dst_t, j0, n)), acts[g][:], gate_t[:, j0 : j0 + n], MULT)
         nc.sync.dma_start(out, out_t[:, :T])

from contextlib import ExitStack

import concourse.mybir as mybir

K, T, E, C, N = 1024, 640, 4, 128, 128
P = 128
S = E * C
FLOPS = 2 * S * K * N

F32 = mybir.dt.float32
BF16 = mybir.dt.bfloat16
U32 = mybir.dt.uint32
I32 = mybir.dt.int32
U16 = mybir.dt.uint16
U8 = mybir.dt.uint8
FP8X4 = mybir.dt.float8_e4m3fn_x4
GELU = mybir.ActivationFunctionType.Gelu_apprx_tanh
COPY = mybir.ActivationFunctionType.Copy
MULT = mybir.AluOpType.mult

PASSES = 2
ROWS = 4
PAIR = 2
PAIRS = PASSES * ROWS // PAIR
LAST = PAIRS - 1
PER_COLUMN = 16
QUADRANT = 32
SCALE_ROWS = 4
EARLY = 2
REST = S - C
GROUPS = ((0, C), (C, REST))
WINDOW = 2 * REST

GPSIMD_TOKENS = 304
SPLIT = 432
GPSIMD_TOKENS_LAST = 328


def tile_moe_two_lin_gelu_kernel(tc, xT, w_words, w_scales, b, gate, offs, dst, out):
    nc = tc.nc
    with ExitStack() as ctx:
        keep = ctx.enter_context(tc.tile_pool(name="keep", bufs=1))
        psum = ctx.enter_context(tc.psum_pool(name="psum", bufs=1))

        offs_t = keep.tile([P, S // PER_COLUMN], U16, name="offs_t")
        dst_t = keep.tile([P, S // PER_COLUMN], U16, name="dst_t")
        b_t = keep.tile([P, E], F32, name="b_t")

        x_rows = xT.rearrange("(a p q r) t -> a q p r t", a=PASSES, q=PAIR, r=PAIR)
        raw = []
        for i in range(PAIRS):
            raw_pair = keep.tile([P, PAIR, T], F32, name=f"raw_pair{i}", align_bytes=64)
            if i < LAST:
                nc.sync.dma_start(raw_pair[:], x_rows[i // PAIR, i % PAIR])
            else:
                run = raw_pair[:].rearrange("p r t -> p (r t)")
                source = x_rows[i // PAIR, i % PAIR].rearrange("p r t -> p (r t)")
                nc.sync.dma_start(run[:, : T + SPLIT], source[:, : T + SPLIT])
                nc.sync.dma_start(run[:, T + SPLIT :], source[:, T + SPLIT :])
            raw.append(raw_pair)
            if i == 0:
                nc.sync.dma_start(offs_t[:], offs)

        w_scale_t = keep.tile([P, PASSES * E, N], U8, name="w_scale_t", align_bytes=64)
        nc.vector.memset(w_scale_t[:].rearrange("p g n -> p (g n)").bitcast(I32), 0)
        out_t = keep.tile([P, WINDOW], F32, name="out_t")
        nc.vector.memset(out_t[:, :T], 0.0)
        warm = keep.tile([P, 1], F32, name="warm")
        nc.vector.memset(warm[:], 0.0)
        nc.scalar.activation(warm[:], warm[:], GELU)

        w_rows = w_words.rearrange("e a p n r -> p (e a) (n r)").bitcast(I32)
        w_early = keep.tile([P, PASSES * EARLY, N], I32, name="w_early", align_bytes=64)
        w_late = keep.tile([P, PASSES * (E - EARLY), N], I32, name="w_late", align_bytes=64)
        nc.sync.dma_start(w_early[:], w_rows[:, : PASSES * EARLY, :])
        for s0 in range(SCALE_ROWS):
            nc.sync.dma_start(
                w_scale_t[s0:P:QUADRANT, :, :].bitcast(I32),
                w_scales[:, :, s0::SCALE_ROWS, :].rearrange("e a s n -> s (e a) n").bitcast(I32),
            )
        nc.sync.dma_start(w_late[:], w_rows[:, PASSES * EARLY :, :])
        nc.sync.dma_start(b_t[:], b)
        gate_t = keep.tile([P, S], F32, name="gate_t")
        nc.sync.dma_start(gate_t[:], gate)
        nc.sync.dma_start(dst_t[:], dst)

        def weights(a, e):
            return w_early[:, PASSES * e + a, :] if e < EARLY else w_late[:, PASSES * (e - EARLY) + a, :]

        token_pairs = [keep.tile([P, T], U32, name=f"token_pairs{i}", align_bytes=64) for i in range(PAIRS)]
        slot_pairs = {
            (a, g): keep.tile([P, PAIR, GROUPS[g][1]], U32, name=f"slot_pairs{a}{g}", align_bytes=64)
            for a, g in ((0, 1), (1, 0), (1, 1))
        }
        woven1 = [keep.tile([P, PAIR * C], U32, name=f"woven1{e}", align_bytes=64) for e in range(E)]
        codes = {
            (1, g): keep.tile([P, n], U32, name=f"codes1{g}", align_bytes=64) for g, (j0, n) in enumerate(GROUPS)
        }
        scales = [
            [keep.tile([P, n], U8, name=f"scales{a}{g}", align_bytes=64) for g, (j0, n) in enumerate(GROUPS)]
            for a in range(PASSES)
        ]

        def round_pair(i):
            target = token_pairs[i][:].bitcast(BF16).rearrange("p (t r) -> p t r", r=PAIR)
            source = raw[i][:].rearrange("p r t -> p t r")
            borders = (GPSIMD_TOKENS, T) if i < LAST else (GPSIMD_TOKENS_LAST, SPLIT, T)
            nc.gpsimd.tensor_copy(target[:, : borders[0], :], source[:, : borders[0], :])
            for t0, t1 in zip(borders, borders[1:]):
                nc.scalar.activation(target[:, t0:t1, :], source[:, t0:t1, :], COPY)

        def entries(list_t, j0, n):
            return list_t[:, j0 // PER_COLUMN : (j0 + n) // PER_COLUMN]

        def place(j0, n):
            g = min(j0 // C, 1)
            return g, slice(j0 - GROUPS[g][0], j0 - GROUPS[g][0] + n)

        def gather(i, j0, n):
            g, cols = place(j0, n)
            nc.vector.tensor_copy(
                slot_pairs[i // PAIR, g][:, i % PAIR, cols], token_pairs[i][:].indirect(entries(offs_t, j0, n))
            )

        def weave(target, a, j0, n):
            g, cols = place(j0, n)
            nc.scalar.copy(
                target.rearrange("p (s q) -> p s q", q=PAIR), slot_pairs[a, g][:, :, cols].rearrange("p q s -> p s q")
            )

        def quantize(a, j0, n, woven):
            g, cols = place(j0, n)
            nc.vector.quantize_mx(
                out=codes[a, g][:, cols].bitcast(FP8X4), scales=scales[a][g][:, cols], in_=woven.bitcast(BF16)
            )

        woven0_first = keep.tile([P, PAIR * C], U32, name="woven0_first", align_bytes=64)
        values = woven0_first[:].bitcast(BF16).rearrange("p (s r) -> p s r", r=ROWS)
        for i in range(PAIR):
            round_pair(i)
            for r in range(PAIR):
                nc.vector.tensor_copy(values[:, :, PAIR * i + r], raw[i][:, r, :].indirect(entries(offs_t, 0, C)))
            gather(i, C, REST)
        codes[0, 0] = keep.tile([P, C], U32, name="raw_pair1", align_bytes=64)
        quantize(0, 0, C, woven0_first[:])

        round_pair(PAIR)
        for j0, n in GROUPS:
            gather(PAIR, j0, n)
        round_pair(LAST)
        woven0_rest = keep.tile([P, PAIR * REST], U32, name=f"raw_pair{LAST}", align_bytes=64)
        weave(woven0_rest[:], 0, C, REST)
        for e in range(E):
            gather(LAST, e * C, C)
            weave(woven1[e][:], 1, e * C, C)
        quantize(1, 0, C, woven1[0][:])
        codes[0, 1] = keep.tile([P, REST], U32, name="slot_pairs10", align_bytes=64)
        quantize(0, C, 2 * C, woven0_rest[:, : PAIR * 2 * C])
        quantize(0, 3 * C, C, woven0_rest[:, PAIR * 2 * C :])
        for e in range(1, E):
            quantize(1, e * C, C, woven1[e][:])

        acts = [keep.tile([P, n], F32, name=f"act{g}") for g, (j0, n) in enumerate(GROUPS)]
        sums = [psum.tile([P, C], F32, name=f"sums{e}") for e in range(E)]
        for j0, n in GROUPS:
            experts = range(j0 // C, (j0 + n) // C)
            for a in range(PASSES):
                for e in experts:
                    g, cols = place(e * C, C)
                    nc.tensor.matmul_mx(
                        out=sums[e][:],
                        lhsT=weights(a, e).bitcast(FP8X4),
                        lhsT_scale=w_scale_t[:, PASSES * e + a, :],
                        rhs=codes[a, g][:, cols].bitcast(FP8X4),
                        rhs_scale=scales[a][g][:, cols],
                        start=(a == 0),
                        stop=(a == PASSES - 1),
                    )
            for e in experts:
                g, cols = place(e * C, C)
                nc.scalar.activation(acts[g][:, cols], sums[e][:], GELU, bias=b_t[:, e : e + 1])

        for g, (j0, n) in enumerate(GROUPS):
            nc.vector.tensor_tensor(out_t[:].indirect(entries(dst_t, j0, n)), acts[g][:], gate_t[:, j0 : j0 + n], MULT)
        nc.sync.dma_start(out, out_t[:, :T])
